import numpy as np
import ml_dtypes


def mxq(x, axis, fmt="e4m3"):
    dtype, down = {"e4m3": (ml_dtypes.float8_e4m3fn, 7), "e5m2": (ml_dtypes.float8_e5m2, 14)}[fmt]
    v = np.moveaxis(np.asarray(x, np.float32).astype(ml_dtypes.bfloat16).astype(np.float64), axis, -1)
    blocks = v.reshape(v.shape[:-1] + (-1, 32))
    amax = np.abs(blocks).max(-1, keepdims=True)
    byte = np.maximum(np.where(amax > 0, np.frexp(amax)[1] - 1 + 127, 0) - down, 1)
    scale = np.exp2(byte - 127.0)
    codes = (blocks / scale).astype(np.float32).astype(dtype).astype(np.float64)
    return np.moveaxis((codes * scale).reshape(v.shape), -1, axis)


WIDE = False


def mx_kscale(k):
    if not WIDE:
        return np.ones(k)
    levels = np.array([10, -10, 5, -5, 0])
    if k % 512:
        return np.exp2(np.random.permutation(np.resize(levels, k // 32))).repeat(32)
    a = np.empty((k // 512, 16))
    for p in range(k // 512):
        a[p, :8] = np.random.permutation(np.resize(levels, 8))
        for g in range(8):
            far = levels[np.abs(levels - a[p, g]) >= 10]
            a[p, g + 8] = far[np.random.randint(len(far))]
    return np.exp2(a.ravel()).repeat(32)


BF16 = ml_dtypes.bfloat16


def bf(x):
    return np.asarray(x, np.float32).astype(BF16)


def f64(x):
    return np.asarray(x).astype(np.float64)


E2M1 = np.array([0.0, 0.5, 1.0, 1.5, 2.0, 3.0, 4.0, 6.0, -0.0, -0.5, -1.0, -1.5, -2.0, -3.0, -4.0, -6.0])


def pack_weight(w, fmt):
    k, n = w.shape
    w = f64(bf(w)).reshape(k // 32, 32, n)
    amax = np.abs(w).max(1)
    if fmt == "e4m3":
        byte = np.frexp(amax)[1] - 1 + 127 - 7
    else:
        mant, ex = np.frexp(amax / 6.0)
        byte = np.where(mant > 0.5, ex, ex - 1) + 127
    byte = np.clip(np.where(amax > 0, byte, 1), 1, 254)
    scaled = (w * np.exp2(127.0 - byte)[:, None, :]).reshape(k, n).astype(np.float32)
    by_word = np.ascontiguousarray(scaled.reshape(k // 512, 128, 4, n).transpose(0, 1, 3, 2))
    if fmt == "e4m3":
        words = by_word.astype(ml_dtypes.float8_e4m3fn).view(np.uint8)
    else:
        c = by_word.astype(ml_dtypes.float4_e2m1fn).view(np.uint8) & 0xF
        words = c[..., 0::2] | (c[..., 1::2] << 4)
    return np.ascontiguousarray(words), np.ascontiguousarray(byte.astype(np.uint8).reshape(k // 512, 16, n))


def unpack_weight(words, scales, fmt):
    g, p, n, _ = words.shape
    if fmt == "e4m3":
        vals = np.ascontiguousarray(words).view(ml_dtypes.float8_e4m3fn).astype(np.float64)
    else:
        nib = np.empty((g, p, n, 4), np.uint8)
        nib[..., 0::2] = words & 0xF
        nib[..., 1::2] = words >> 4
        vals = E2M1[nib]
    vals = vals * np.repeat(np.exp2(scales.astype(np.float64) - 127.0), 8, axis=1)[..., None]
    return vals.transpose(0, 1, 3, 2).reshape(g * 512, n)
def pack4(w):
    words, scales = pack_weight(w, "e2m1")
    return words.reshape(words.shape[0], 128, -1), scales


def unpack4(words, scales):
    return unpack_weight(words.reshape(words.shape[0], 128, -1, 2), scales, "e2m1")


def planes(Y):
    n, m = Y.shape
    b = f64(bf(Y)).reshape(n // 32, 32, m)
    amax = np.abs(b).max(1)
    byte = np.clip(np.where(amax > 0, np.frexp(amax)[1] - 1 + 127 - 7, 1), 1, 254)
    codes = (b * np.exp2(127.0 - byte)[:, None, :]).reshape(n, m).astype(np.float32).astype(ml_dtypes.float8_e4m3fn).view(np.uint8)
    words = codes.reshape(n // 512, 128, 4, m).transpose(0, 1, 3, 2)
    return np.ascontiguousarray(words), np.ascontiguousarray(byte.astype(np.uint8).reshape(n // 512, 16, m))


G, R, K, B, D = 4, 512, 512, 1024, 1024
SHARP = 2.0

def setup_inputs():
    s = mx_kscale(G * K)
    t = mx_kscale(G * B)
    x = np.random.randn(G, R, K) * s.reshape(G, 1, K)
    H = SHARP * np.random.randn(G * K, B) / np.sqrt(K) / s[:, None]
    C = np.where(np.random.rand(G * B, D) < 0.5, -1.0, 1.0) / np.sqrt(B) / t[:, None]
    h_words, h_scales = pack4(H)
    c_words, c_scales = pack4(C)
    bit_gain = np.exp(0.3 * np.random.randn(G, B)) * t.reshape(G, B)
    lex = 0.5 * np.random.randn(G, R, D)
    doc_gain = np.exp(0.8 * np.random.randn(G, D))
    doc_bias = 0.3 * np.random.randn(G, D)
    return {"x": bf(x), "h_words": h_words, "h_scales": h_scales, "bit_gain": bf(bit_gain),
            "c_words": c_words, "c_scales": c_scales, "lex": bf(lex),
            "doc_gain": bf(doc_gain), "doc_bias": bf(doc_bias)}

def reference(x, h_words, h_scales, bit_gain, c_words, c_scales, lex, doc_gain, doc_bias):
    H = unpack4(h_words, h_scales).reshape(G, K, B)
    C = unpack4(c_words, c_scales).reshape(G, B, D)
    P = mxq(f64(x), 2) @ H
    Z = np.tanh(P) * f64(bit_gain)[:, None, :]
    S = mxq(Z, 2) @ C
    y = (S + f64(lex)) * f64(doc_gain)[:, None, :] + f64(doc_bias)[:, None, :]
    Y = y.transpose(2, 0, 1).reshape(D, G * R)
    words, scales = planes(Y)
    return y, words, scales

@@ -1,0 +1,343 @@
+from contextlib import ExitStack
+
+import concourse.mybir as mybir
+from concourse.masks import make_identity
+
+G, R, K, B, D = 4, 512, 512, 1024, 1024
+FLOPS = 2 * G * R * (K * B + B * D)
+
+F32 = mybir.dt.float32
+BF16 = mybir.dt.bfloat16
+I32 = mybir.dt.int32
+U32 = mybir.dt.uint32
+U8 = mybir.dt.uint8
+FP8X4 = mybir.dt.float8_e4m3fn_x4
+FP4X4 = mybir.dt.float4_e2m1fn_x4
+ACT = mybir.ActivationFunctionType
+ALU = mybir.AluOpType
+
+P = 128
+PACK = 4
+KP = P * PACK
+HALF = 256
+HALVES = G * R // HALF
+STEPS = 2 * HALVES
+BANKS = 8
+LAG_S, LAG_T, LAG_B = 3, 4, 5
+
+
+def tile_soft_hyperplane_hash_scores_k7_kernel(
+    tc, x, h_words, h_scales, bit_gain, c_words, c_scales, lex, doc_gain, doc_bias, out_0, out_1, out_2
+):
+    nc = tc.nc
+    with ExitStack() as ctx:
+        keep = ctx.enter_context(tc.tile_pool(name="keep", bufs=1))
+        work = ctx.enter_context(tc.tile_pool(name="work", bufs=3))
+        psum = ctx.enter_context(tc.psum_pool(name="psum", bufs=1))
+        ctx.enter_context(tc.manual_schedule())
+
+        bank_uses = []
+
+        def next_bank():
+            n = len(bank_uses)
+            bank_uses.append(n)
+            return psum.tile([P, KP], F32, name="bank%d" % n, tag="bank%d" % (n % BANKS))
+
+        ident = keep.tile([P, P], F32, name="ident")
+        make_identity(nc, ident[:])
+
+        warm = keep.tile([P, 1], F32, name="warm")
+        nc.scalar.activation(out=warm[:], in_=ident[:, 0:1], func=ACT.Tanh)
+
+        h_plane = keep.tile([P, G, B], U8, name="h_plane", align_bytes=64)
+        c_plane = keep.tile([P, 2 * G, D], U8, name="c_plane", align_bytes=64)
+        nc.vector.memset(h_plane[:].rearrange("p v n -> p (v n)").bitcast(I32), 0)
+        nc.vector.memset(c_plane[:].rearrange("p v n -> p (v n)").bitcast(I32), 0)
+
+        x_sb = [keep.tile([P, 2, K], BF16, name="x%d" % h) for h in range(HALVES)]
+        lex_sb = [keep.tile([P, 2, D], BF16, name="lex%d" % h) for h in range(HALVES)]
+        h_sb = [keep.tile([P, 2 * B], U8, name="h%d" % v) for v in range(G)]
+        c_sb = [keep.tile([P, 2, 2 * D], U8, name="c%d" % v, align_bytes=64) for v in range(G)]
+        gain = keep.tile([P, 2 * G, PACK], BF16, name="gain")
+        dgain_bf = keep.tile([P, 2 * G, PACK], BF16, name="dgain_bf")
+        dbias_bf = keep.tile([P, 2 * G, PACK], BF16, name="dbias_bf")
+        dgain = keep.tile([P, 2 * G, PACK], F32, name="dgain")
+        dbias = keep.tile([P, 2 * G, PACK], F32, name="dbias")
+        y_scales = keep.tile([P, 2, G * R], U8, name="y_scales", align_bytes=64)
+
+        def rows(t, h):
+            v, r0 = h // 2, (h % 2) * HALF
+            return t[v, r0 : r0 + HALF, :].rearrange("(b r) k -> r b k", b=2)
+
+        def load_x(h):
+            nc.sync.dma_start(out=x_sb[h][:], in_=rows(x, h))
+
+        def load_lex(h):
+            nc.sync.dma_start(out=lex_sb[h][:], in_=rows(lex, h))
+
+        def load_h(v):
+            nc.sync.dma_start(out=h_sb[v][:].bitcast(I32), in_=h_words[v].bitcast(I32))
+
+        def load_c(v):
+            nc.sync.dma_start(
+                out=c_sb[v][:].bitcast(I32), in_=c_words[2 * v : 2 * v + 2].rearrange("g p n -> p g n").bitcast(I32)
+            )
+
+        def load_plane(plane, scales):
+            for q in range(4):
+                nc.sync.dma_start(
+                    out=plane[32 * q : 32 * q + 4].bitcast(I32),
+                    in_=scales[:, 4 * q : 4 * q + 4, :].rearrange("g r n -> r g n").bitcast(I32),
+                )
+
+        def load_vec(tile, vec):
+            nc.sync.dma_start(out=tile[:], in_=vec.rearrange("v (g p t) -> p (v g) t", g=2, t=PACK))
+
+        load_x(0)
+        load_h(0)
+        load_plane(h_plane, h_scales)
+        load_vec(gain, bit_gain)
+        load_x(1)
+        load_plane(c_plane, c_scales)
+        load_c(0)
+        load_vec(dgain_bf, doc_gain)
+        load_vec(dbias_bf, doc_bias)
+        load_lex(0)
+        for v in range(1, G):
+            load_h(v)
+            load_x(2 * v)
+            load_lex(2 * v - 1)
+            load_x(2 * v + 1)
+            load_c(v)
+            load_lex(2 * v)
+        load_lex(HALVES - 1)
+
+        x_bank, x_grouped, x_q, h_perm, p_bank, tanh_sb, z_bf, z_q = {}, {}, {}, {}, {}, {}, {}, {}
+        s_bank, sum_sb, t_bank, y_t, b_bank, y_bf = {}, {}, {}, {}, {}, {}
+
+        def turn_x(h):
+            bank = next_bank()
+            for b in range(2):
+                words = x_sb[h][:, b, :].bitcast(F32)
+                for u in range(2):
+                    j = 2 * b + u
+                    nc.tensor.transpose(bank[:, j * P : (j + 1) * P], words[:, u : 2 * P : 2], ident[:])
+            x_bank[h] = bank
+
+        def copy_x(h):
+            t = work.tile([P, HALF * PACK], BF16, name="xg%d" % h, tag="xg", bufs=2, align_bytes=64)
+            nc.scalar.copy(
+                out=t[:].bitcast(F32).rearrange("p (b r u) -> p b r u", b=2, u=2),
+                in_=x_bank[h][:].rearrange("p (b u r) -> p b r u", b=2, u=2),
+            )
+            x_grouped[h] = t
+
+        def quantize(src, tag, n, bufs):
+            codes = work.tile([P, HALF], U32, name="%s_q%d" % (tag, n), tag=tag + "_q", bufs=bufs, align_bytes=64)
+            scales = work.tile([P, HALF], U8, name="%s_s%d" % (tag, n), tag=tag + "_s", bufs=bufs, align_bytes=64)
+            nc.vector.quantize_mx(out=codes[:].bitcast(FP8X4), scales=scales[:], in_=src[:])
+            return codes, scales
+
+        def quantize_x(h):
+            x_q[h] = quantize(x_grouped[h], "x", h, 3)
+
+        def permute_h(v, g):
+            n = 2 * v + g
+            words = work.tile([P, 2 * KP], U8, name="hw%d" % n, tag="hw", bufs=4, align_bytes=64)
+            scales = work.tile([P, KP], U8, name="hs%d" % n, tag="hs", bufs=4, align_bytes=64)
+            nc.vector.tensor_copy(
+                out=words[:].rearrange("p (t m b) -> p t m b", t=PACK, b=2),
+                in_=h_sb[v][:, 2 * KP * g : 2 * KP * (g + 1)].rearrange("p (m t b) -> p t m b", t=PACK, b=2),
+            )
+            nc.vector.tensor_copy(
+                out=scales[:].rearrange("p (t m) -> p t m", t=PACK),
+                in_=h_plane[:, v, KP * g : KP * (g + 1)].rearrange("p (m t) -> p t m", t=PACK),
+            )
+            h_perm[n] = (words, scales)
+
+        def project(s):
+            h, g = divmod(s, 2)
+            words, scales = h_perm[2 * (h // 2) + g]
+            codes, code_scales = x_q[h]
+            for u in range(2):
+                bank = next_bank()
+                for e in range(2):
+                    t = 2 * u + e
+                    nc.tensor.matmul_mx(
+                        out=bank[:, e * HALF : (e + 1) * HALF],
+                        lhsT=words[:, 2 * P * t : 2 * P * (t + 1)].bitcast(FP4X4),
+                        lhsT_scale=scales[:, P * t : P * (t + 1)],
+                        rhs=codes[:].bitcast(FP8X4),
+                        rhs_scale=code_scales[:],
+                        start=True,
+                        stop=True,
+                    )
+                p_bank[s, u] = bank
+
+        def soften(s):
+            t = work.tile([P, 2, HALF, 2], F32, name="tanh%d" % s, tag="tanh")
+            for u in range(2):
+                nc.scalar.activation(
+                    out=t[:, u], in_=p_bank[s, u][:].rearrange("p (e r) -> p r e", e=2), func=ACT.Tanh
+                )
+            tanh_sb[s] = t
+
+        def apply_gain(s):
+            h, g = divmod(s, 2)
+            t = work.tile([P, HALF * PACK], BF16, name="z%d" % s, tag="z", bufs=2, align_bytes=64)
+            factor = gain[:, 2 * (h // 2) + g, :].rearrange("p (u e) -> p u e", u=2)
+            nc.vector.tensor_tensor(
+                out=t[:].rearrange("p (r u e) -> p r u e", u=2, e=2),
+                in0=tanh_sb[s][:].rearrange("p u r e -> p r u e"),
+                in1=factor.unsqueeze(1).to_broadcast([P, HALF, 2, 2]),
+                op=ALU.mult,
+            )
+            z_bf[s] = t
+
+        def quantize_z(s):
+            z_q[s] = quantize(z_bf[s], "z", s, 6)
+
+        def score(s):
+            h, dh = divmod(s, 2)
+            v = h // 2
+            for b in range(2):
+                bank = next_bank()
+                for g in range(2):
+                    codes, scales = z_q[2 * h + g]
+                    nc.tensor.matmul_mx(
+                        out=bank[:],
+                        lhsT=codes[:, b * P : (b + 1) * P].bitcast(FP8X4),
+                        lhsT_scale=scales[:, b * P : (b + 1) * P],
+                        rhs=c_sb[v][:, g, 2 * KP * dh : 2 * KP * (dh + 1)].bitcast(FP4X4),
+                        rhs_scale=c_plane[:, 2 * v + g, KP * dh : KP * (dh + 1)],
+                        start=(g == 0),
+                        stop=(g == 1),
+                    )
+                s_bank[s, b] = bank
+
+        def add_lex(s):
+            h, dh = divmod(s, 2)
+            t = work.tile([P, 2, KP], F32, name="sum%d" % s, tag="sum")
+            for b in range(2):
+                nc.vector.tensor_tensor(
+                    out=t[:, b, :].rearrange("r (t c i) -> r c t i", t=PACK, i=4),
+                    in0=s_bank[s, b][:].rearrange("r (c i t) -> r c t i", t=PACK, i=4),
+                    in1=lex_sb[h][:, b, KP * dh : KP * (dh + 1)].rearrange("r (c i t) -> r c t i", t=PACK, i=4),
+                    op=ALU.add,
+                )
+            sum_sb[s] = t
+
+        def turn_sum(s):
+            for u in range(2):
+                bank = next_bank()
+                for e in range(2):
+                    t = 2 * u + e
+                    for b in range(2):
+                        j = 2 * e + b
+                        nc.tensor.transpose(bank[:, j * P : (j + 1) * P], sum_sb[s][:, b, t * P : (t + 1) * P], ident[:])
+                t_bank[s, u] = bank
+
+        def finish(s):
+            h, dh = divmod(s, 2)
+            n = 2 * (h // 2) + dh
+            y = work.tile([P, PACK, HALF], F32, name="yt%d" % s, tag="yt")
+            for t in range(PACK):
+                u, e = divmod(t, 2)
+                src = t_bank[s, u][:, e * HALF : (e + 1) * HALF]
+                scale, bias = dgain[:, n, t : t + 1], dbias[:, n, t : t + 1]
+                if u == 1 and s >= STEPS - 2:
+                    nc.vector.tensor_scalar(
+                        out=y[:, t, :], in0=src, scalar1=scale, scalar2=bias, op0=ALU.mult, op1=ALU.add
+                    )
+                else:
+                    nc.scalar.activation(out=y[:, t, :], in_=src, func=ACT.Identity, scale=scale, bias=bias)
+            y_t[s] = y
+
+        def turn_back(s):
+            for b in range(2):
+                bank = next_bank()
+                for t in range(PACK):
+                    nc.tensor.transpose(bank[:, t * P : (t + 1) * P], y_t[s][:, t, b * P : (b + 1) * P], ident[:])
+                b_bank[s, b] = bank
+
+        def store_y(s):
+            h, dh = divmod(s, 2)
+            for b in range(2):
+                y = work.tile([P, KP], F32, name="y%d_%d" % (s, b), tag="y", bufs=4)
+                nc.scalar.copy(
+                    out=y[:].rearrange("r (p t) -> r p t", t=PACK),
+                    in_=b_bank[s, b][:].rearrange("r (t p) -> r p t", t=PACK),
+                )
+                r0 = (h % 2) * HALF + b * P
+                nc.sync.dma_start(out=out_0[h // 2, r0 : r0 + P, KP * dh : KP * (dh + 1)], in_=y[:])
+
+        def group_y(s):
+            t = work.tile([P, HALF * PACK], BF16, name="yb%d" % s, tag="yb", bufs=2, align_bytes=64)
+            nc.vector.tensor_copy(
+                out=t[:].rearrange("p (c i t) -> p c t i", t=PACK, i=2),
+                in_=y_t[s][:].rearrange("p t (c i) -> p c t i", i=2),
+            )
+            y_bf[s] = t
+
+        def quantize_y(s):
+            h, dh = divmod(s, 2)
+            cols = slice(h * HALF, (h + 1) * HALF)
+            codes = work.tile([P, HALF], U32, name="yq%d" % s, tag="yq", align_bytes=64)
+            nc.vector.quantize_mx(out=codes[:].bitcast(FP8X4), scales=y_scales[:, dh, cols], in_=y_bf[s][:])
+            nc.sync.dma_start(
+                out=out_1[dh, :, cols, :].rearrange("p m t -> p (m t)").bitcast(I32), in_=codes[:].bitcast(I32)
+            )
+            if s % 4 == 3:
+                view = slice((h // 2) * R, (h // 2 + 1) * R)
+                for q in range(4):
+                    nc.sync.dma_start(
+                        out=out_2[:, 4 * q : 4 * q + 4, view].rearrange("g r m -> r g m").bitcast(I32),
+                        in_=y_scales[32 * q : 32 * q + 4, :, view].bitcast(I32),
+                    )
+
+        def live(s):
+            return 0 <= s < STEPS
+
+        turn_x(0)
+        permute_h(0, 0)
+        copy_x(0)
+        quantize_x(0)
+        permute_h(0, 1)
+
+        for step in range(STEPS + LAG_B):
+            s_s, s_t, s_b = step - LAG_S, step - LAG_T, step - LAG_B
+            next_half = step // 2 + 1
+            if live(s_s):
+                score(s_s)
+            if live(step):
+                project(step)
+            if step % 2 == 0 and next_half < HALVES:
+                turn_x(next_half)
+            if live(s_t):
+                turn_sum(s_t)
+            if live(s_b):
+                turn_back(s_b)
+            if live(step):
+                soften(step)
+            if live(s_s):
+                add_lex(s_s)
+            if live(step - 1):
+                quantize_z(step - 1)
+            if step % 2 == 0 and next_half < HALVES:
+                copy_x(next_half)
+            if live(s_b):
+                group_y(s_b)
+            if step % 2 == 1 and next_half < HALVES:
+                quantize_x(next_half)
+            if step % 2 == 1 and (step + 3) // 4 < G:
+                permute_h((step + 3) // 4, ((step + 3) // 2) % 2)
+            if live(step):
+                apply_gain(step)
+            if step == LAG_T - 1:
+                nc.vector.tensor_copy(out=dgain[:], in_=dgain_bf[:])
+                nc.vector.tensor_copy(out=dbias[:], in_=dbias_bf[:])
+            if live(s_t):
+                finish(s_t)
+            if live(s_b):
+                quantize_y(s_b)
+                store_y(s_b)

@@ -24,6 +24,7 @@ HALVES = G * R // HALF
 STEPS = 2 * HALVES
 BANKS = 8
 LAG_S, LAG_T, LAG_B = 3, 4, 5
+GROUP_ON_SCALAR = (3, 7)
 
 
 def tile_soft_hyperplane_hash_scores_k7_kernel(
@@ -43,26 +44,29 @@ def tile_soft_hyperplane_hash_scores_k7_kernel(
             bank_uses.append(n)
             return psum.tile([P, KP], F32, name="bank%d" % n, tag="bank%d" % (n % BANKS))
 
+        vec_rows = keep.tile([P, KP], BF16, name="vec_rows")
+        nc.gpsimd.memset(vec_rows[:].bitcast(I32), 0)
         ident = keep.tile([P, P], F32, name="ident")
         make_identity(nc, ident[:])
 
         warm = keep.tile([P, 1], F32, name="warm")
         nc.scalar.activation(out=warm[:], in_=ident[:, 0:1], func=ACT.Tanh)
 
-        h_plane = keep.tile([P, G, B], U8, name="h_plane", align_bytes=64)
-        c_plane = keep.tile([P, 2 * G, D], U8, name="c_plane", align_bytes=64)
-        nc.vector.memset(h_plane[:].rearrange("p v n -> p (v n)").bitcast(I32), 0)
-        nc.vector.memset(c_plane[:].rearrange("p v n -> p (v n)").bitcast(I32), 0)
+        h_first = keep.tile([P, 1, B], U8, name="h_first", align_bytes=64)
+        h_rest = keep.tile([P, G - 1, B], U8, name="h_rest", align_bytes=64)
+        c_first = keep.tile([P, 2, D], U8, name="c_first", align_bytes=64)
+        c_rest = keep.tile([P, 2 * (G - 1), D], U8, name="c_rest", align_bytes=64)
+        for plane in (h_first, h_rest, c_first, c_rest):
+            nc.vector.memset(plane[:].rearrange("p v n -> p (v n)").bitcast(I32), 0)
+        h_plane = [h_first[:, 0, :]] + [h_rest[:, n, :] for n in range(G - 1)]
+        c_plane = [c_first[:, n, :] for n in range(2)] + [c_rest[:, n, :] for n in range(2 * (G - 1))]
 
         x_sb = [keep.tile([P, 2, K], BF16, name="x%d" % h) for h in range(HALVES)]
         lex_sb = [keep.tile([P, 2, D], BF16, name="lex%d" % h) for h in range(HALVES)]
         h_sb = [keep.tile([P, 2 * B], U8, name="h%d" % v) for v in range(G)]
         c_sb = [keep.tile([P, 2, 2 * D], U8, name="c%d" % v, align_bytes=64) for v in range(G)]
-        gain = keep.tile([P, 2 * G, PACK], BF16, name="gain")
-        dgain_bf = keep.tile([P, 2 * G, PACK], BF16, name="dgain_bf")
-        dbias_bf = keep.tile([P, 2 * G, PACK], BF16, name="dbias_bf")
-        dgain = keep.tile([P, 2 * G, PACK], F32, name="dgain")
-        dbias = keep.tile([P, 2 * G, PACK], F32, name="dbias")
+        vecs = keep.tile([P, 3 * 2 * G, PACK], F32, name="vecs")
+        gain, dgain, dbias = [vecs[:, 2 * G * n : 2 * G * (n + 1), :] for n in range(3)]
         y_scales = keep.tile([P, 2, G * R], U8, name="y_scales", align_bytes=64)
 
         def rows(t, h):
@@ -90,27 +94,40 @@ def tile_soft_hyperplane_hash_scores_k7_kernel(
                     in_=scales[:, 4 * q : 4 * q + 4, :].rearrange("g r n -> r g n").bitcast(I32),
                 )
 
-        def load_vec(tile, vec):
-            nc.sync.dma_start(out=tile[:], in_=vec.rearrange("v (g p t) -> p (v g) t", g=2, t=PACK))
-
         load_x(0)
         load_h(0)
-        load_plane(h_plane, h_scales)
-        load_vec(gain, bit_gain)
+        load_plane(h_first, h_scales[0:1])
+        for n, vec in enumerate((bit_gain, doc_gain, doc_bias)):
+            nc.sync.dma_start(
+                out=vec_rows[2 * G * n : 2 * G * (n + 1), :], in_=vec.rearrange("v (g k) -> (v g) k", g=2)
+            )
         load_x(1)
-        load_plane(c_plane, c_scales)
+        load_h(1)
+        load_x(2)
+        load_plane(h_rest, h_scales[1:G])
+        load_plane(c_first, c_scales[0:2])
         load_c(0)
-        load_vec(dgain_bf, doc_gain)
-        load_vec(dbias_bf, doc_bias)
         load_lex(0)
+        load_x(3)
+        load_lex(1)
+        load_plane(c_rest, c_scales[2 : 2 * G])
         for v in range(1, G):
-            load_h(v)
-            load_x(2 * v)
-            load_lex(2 * v - 1)
-            load_x(2 * v + 1)
             load_c(v)
+            if v + 1 < G:
+                load_h(v + 1)
+                load_x(2 * v + 2)
             load_lex(2 * v)
-        load_lex(HALVES - 1)
+            if v + 1 < G:
+                load_x(2 * v + 3)
+            load_lex(2 * v + 1)
+
+        def turn_vecs():
+            bank = next_bank()
+            words = vec_rows[:].bitcast(F32)
+            for u in range(2):
+                nc.tensor.transpose(bank[:, u * P : (u + 1) * P], words[:, u : 2 * P : 2], ident[:])
+            turned = bank[:, 0 : 2 * P].bitcast(BF16).rearrange("p (u j e) -> p j u e", u=2, e=2)
+            nc.scalar.copy(out=vecs[:].rearrange("p j (u e) -> p j u e", u=2), in_=turned[:, 0 : 3 * 2 * G])
 
         x_bank, x_grouped, x_q, h_perm, p_bank, tanh_sb, z_bf, z_q = {}, {}, {}, {}, {}, {}, {}, {}
         s_bank, sum_sb, t_bank, y_t, b_bank, y_bf = {}, {}, {}, {}, {}, {}
@@ -132,32 +149,33 @@ def tile_soft_hyperplane_hash_scores_k7_kernel(
             )
             x_grouped[h] = t
 
-        def quantize(src, tag, n, bufs):
-            codes = work.tile([P, HALF], U32, name="%s_q%d" % (tag, n), tag=tag + "_q", bufs=bufs, align_bytes=64)
-            scales = work.tile([P, HALF], U8, name="%s_s%d" % (tag, n), tag=tag + "_s", bufs=bufs, align_bytes=64)
+        def quantize(src, width, tag, n, bufs):
+            codes = work.tile([P, width], U32, name="%s_q%d" % (tag, n), tag=tag + "_q", bufs=bufs, align_bytes=64)
+            scales = work.tile([P, width], U8, name="%s_s%d" % (tag, n), tag=tag + "_s", bufs=bufs, align_bytes=64)
             nc.vector.quantize_mx(out=codes[:].bitcast(FP8X4), scales=scales[:], in_=src[:])
             return codes, scales
 
         def quantize_x(h):
-            x_q[h] = quantize(x_grouped[h], "x", h, 3)
+            x_q[h] = quantize(x_grouped[h], HALF, "x", h, 3)
 
-        def permute_h(v, g):
-            n = 2 * v + g
-            words = work.tile([P, 2 * KP], U8, name="hw%d" % n, tag="hw", bufs=4, align_bytes=64)
-            scales = work.tile([P, KP], U8, name="hs%d" % n, tag="hs", bufs=4, align_bytes=64)
+        h_words_perm = [keep.tile([P, PACK, 2 * P, 2], U8, name="hw%d" % v, align_bytes=64) for v in range(G)]
+        h_scales_perm = [keep.tile([P, PACK, 2 * P], U8, name="hs%d" % v, align_bytes=64) for v in range(G)]
+
+        def permute_words(v, m0, m1):
             nc.vector.tensor_copy(
-                out=words[:].rearrange("p (t m b) -> p t m b", t=PACK, b=2),
-                in_=h_sb[v][:, 2 * KP * g : 2 * KP * (g + 1)].rearrange("p (m t b) -> p t m b", t=PACK, b=2),
+                out=h_words_perm[v][:, :, m0:m1, :],
+                in_=h_sb[v][:].rearrange("p (m t b) -> p t m b", t=PACK, b=2)[:, :, m0:m1, :],
             )
+
+        def permute_scales(v, m0, m1):
             nc.vector.tensor_copy(
-                out=scales[:].rearrange("p (t m) -> p t m", t=PACK),
-                in_=h_plane[:, v, KP * g : KP * (g + 1)].rearrange("p (m t) -> p t m", t=PACK),
+                out=h_scales_perm[v][:, :, m0:m1], in_=h_plane[v].rearrange("p (m t) -> p t m", t=PACK)[:, :, m0:m1]
             )
-            h_perm[n] = (words, scales)
 
         def project(s):
             h, g = divmod(s, 2)
-            words, scales = h_perm[2 * (h // 2) + g]
+            words = h_words_perm[h // 2][:].rearrange("p t m b -> p t (m b)")
+            scales = h_scales_perm[h // 2]
             codes, code_scales = x_q[h]
             for u in range(2):
                 bank = next_bank()
@@ -165,8 +183,8 @@ def tile_soft_hyperplane_hash_scores_k7_kernel(
                     t = 2 * u + e
                     nc.tensor.matmul_mx(
                         out=bank[:, e * HALF : (e + 1) * HALF],
-                        lhsT=words[:, 2 * P * t : 2 * P * (t + 1)].bitcast(FP4X4),
-                        lhsT_scale=scales[:, P * t : P * (t + 1)],
+                        lhsT=words[:, t, 2 * P * g : 2 * P * (g + 1)].bitcast(FP4X4),
+                        lhsT_scale=scales[:, t, P * g : P * (g + 1)],
                         rhs=codes[:].bitcast(FP8X4),
                         rhs_scale=code_scales[:],
                         start=True,
@@ -175,7 +193,7 @@ def tile_soft_hyperplane_hash_scores_k7_kernel(
                 p_bank[s, u] = bank
 
         def soften(s):
-            t = work.tile([P, 2, HALF, 2], F32, name="tanh%d" % s, tag="tanh")
+            t = work.tile([P, 2, HALF, 2], F32, name="tanh%d" % s, tag="tanh", bufs=4)
             for u in range(2):
                 nc.scalar.activation(
                     out=t[:, u], in_=p_bank[s, u][:].rearrange("p (e r) -> p r e", e=2), func=ACT.Tanh
@@ -184,18 +202,19 @@ def tile_soft_hyperplane_hash_scores_k7_kernel(
 
         def apply_gain(s):
             h, g = divmod(s, 2)
-            t = work.tile([P, HALF * PACK], BF16, name="z%d" % s, tag="z", bufs=2, align_bytes=64)
+            if g == 0:
+                z_bf[h] = work.tile([P, 2 * HALF * PACK], BF16, name="z%d" % h, tag="z", bufs=2, align_bytes=64)
+            t = z_bf[h][:, g * HALF * PACK : (g + 1) * HALF * PACK]
             factor = gain[:, 2 * (h // 2) + g, :].rearrange("p (u e) -> p u e", u=2)
             nc.vector.tensor_tensor(
-                out=t[:].rearrange("p (r u e) -> p r u e", u=2, e=2),
+                out=t.rearrange("p (r u e) -> p r u e", u=2, e=2),
                 in0=tanh_sb[s][:].rearrange("p u r e -> p r u e"),
                 in1=factor.unsqueeze(1).to_broadcast([P, HALF, 2, 2]),
                 op=ALU.mult,
             )
-            z_bf[s] = t
 
-        def quantize_z(s):
-            z_q[s] = quantize(z_bf[s], "z", s, 6)
+        def quantize_z(h):
+            z_q[h] = quantize(z_bf[h], 2 * HALF, "z", h, 3)
 
         def score(s):
             h, dh = divmod(s, 2)
@@ -203,29 +222,31 @@ def tile_soft_hyperplane_hash_scores_k7_kernel(
             for b in range(2):
                 bank = next_bank()
                 for g in range(2):
-                    codes, scales = z_q[2 * h + g]
+                    codes, scales = z_q[h]
+                    cols = slice(g * HALF + b * P, g * HALF + (b + 1) * P)
                     nc.tensor.matmul_mx(
                         out=bank[:],
-                        lhsT=codes[:, b * P : (b + 1) * P].bitcast(FP8X4),
-                        lhsT_scale=scales[:, b * P : (b + 1) * P],
+                        lhsT=codes[:, cols].bitcast(FP8X4),
+                        lhsT_scale=scales[:, cols],
                         rhs=c_sb[v][:, g, 2 * KP * dh : 2 * KP * (dh + 1)].bitcast(FP4X4),
-                        rhs_scale=c_plane[:, 2 * v + g, KP * dh : KP * (dh + 1)],
+                        rhs_scale=c_plane[2 * v + g][:, KP * dh : KP * (dh + 1)],
                         start=(g == 0),
                         stop=(g == 1),
                     )
                 s_bank[s, b] = bank
 
-        def add_lex(s):
+        def add_lex(s, b):
             h, dh = divmod(s, 2)
-            t = work.tile([P, 2, KP], F32, name="sum%d" % s, tag="sum")
-            for b in range(2):
+            if b == 0:
+                sum_sb[s] = work.tile([P, 2, KP], F32, name="sum%d" % s, tag="sum")
+            t = sum_sb[s]
+            for t in (t,):
                 nc.vector.tensor_tensor(
                     out=t[:, b, :].rearrange("r (t c i) -> r c t i", t=PACK, i=4),
                     in0=s_bank[s, b][:].rearrange("r (c i t) -> r c t i", t=PACK, i=4),
                     in1=lex_sb[h][:, b, KP * dh : KP * (dh + 1)].rearrange("r (c i t) -> r c t i", t=PACK, i=4),
                     op=ALU.add,
                 )
-            sum_sb[s] = t
 
         def turn_sum(s):
             for u in range(2):
@@ -273,9 +294,10 @@ def tile_soft_hyperplane_hash_scores_k7_kernel(
 
         def group_y(s):
             t = work.tile([P, HALF * PACK], BF16, name="yb%d" % s, tag="yb", bufs=2, align_bytes=64)
-            nc.vector.tensor_copy(
-                out=t[:].rearrange("p (c i t) -> p c t i", t=PACK, i=2),
-                in_=y_t[s][:].rearrange("p t (c i) -> p c t i", i=2),
+            copy = nc.scalar.copy if s in GROUP_ON_SCALAR else nc.vector.tensor_copy
+            copy(
+                out=t[:].rearrange("p (c i t) -> p c t i", t=PACK, i=4),
+                in_=y_t[s][:].rearrange("p t (c i) -> p c t i", i=4),
             )
             y_bf[s] = t
 
@@ -298,44 +320,59 @@ def tile_soft_hyperplane_hash_scores_k7_kernel(
         def live(s):
             return 0 <= s < STEPS
 
+        def project_step(s):
+            return s if s <= 2 else s - 1
+
+        def due(first, lead, step):
+            return max(0, project_step(first) - lead) == step
+
         turn_x(0)
-        permute_h(0, 0)
+        permute_words(0, 0, P)
+        turn_vecs()
         copy_x(0)
+        permute_scales(0, 0, P)
         quantize_x(0)
-        permute_h(0, 1)
+        permute_words(0, P, 2 * P)
+        permute_scales(0, P, 2 * P)
 
         for step in range(STEPS + LAG_B):
             s_s, s_t, s_b = step - LAG_S, step - LAG_T, step - LAG_B
-            next_half = step // 2 + 1
+            projected = [s for s in range(STEPS) if project_step(s) == step]
+            turned = [h for h in range(1, HALVES) if due(2 * h, 2, step)]
             if live(s_s):
                 score(s_s)
-            if live(step):
-                project(step)
-            if step % 2 == 0 and next_half < HALVES:
-                turn_x(next_half)
+            for s in projected:
+                project(s)
+            for h in turned:
+                turn_x(h)
             if live(s_t):
                 turn_sum(s_t)
             if live(s_b):
                 turn_back(s_b)
-            if live(step):
-                soften(step)
-            if live(s_s):
-                add_lex(s_s)
-            if live(step - 1):
-                quantize_z(step - 1)
-            if step % 2 == 0 and next_half < HALVES:
-                copy_x(next_half)
-            if live(s_b):
+            if live(s_b) and s_b in GROUP_ON_SCALAR:
                 group_y(s_b)
-            if step % 2 == 1 and next_half < HALVES:
-                quantize_x(next_half)
-            if step % 2 == 1 and (step + 3) // 4 < G:
-                permute_h((step + 3) // 4, ((step + 3) // 2) % 2)
+            for s in projected:
+                soften(s)
+            for h in turned:
+                copy_x(h)
+            if live(s_s):
+                add_lex(s_s, 0)
+            if live(step - 1) and step % 2 == 0:
+                quantize_z(step // 2 - 1)
+            if live(s_b) and s_b not in GROUP_ON_SCALAR:
+                group_y(s_b)
+            if live(s_s):
+                add_lex(s_s, 1)
+            for h in range(1, HALVES):
+                if due(2 * h, 1, step):
+                    quantize_x(h)
+            for v in range(1, G):
+                if due(4 * v, 2, step):
+                    permute_words(v, 0, 2 * P)
+                if due(4 * v, 1, step):
+                    permute_scales(v, 0, 2 * P)
             if live(step):
                 apply_gain(step)
-            if step == LAG_T - 1:
-                nc.vector.tensor_copy(out=dgain[:], in_=dgain_bf[:])
-                nc.vector.tensor_copy(out=dbias[:], in_=dbias_bf[:])
             if live(s_t):
                 finish(s_t)
             if live(s_b):

@@ -23,8 +23,10 @@ HALF = 256
 HALVES = G * R // HALF
 STEPS = 2 * HALVES
 BANKS = 8
-LAG_S, LAG_T, LAG_B = 3, 4, 5
-GROUP_ON_SCALAR = (3, 7)
+LAG_S, LAG_T, LAG_G, LAG_B = 3, 4, 5, 6
+GROUP_ON_SCALAR = (0,)
+WORDS_STEP = {1: 0, 2: 5, 3: 9}
+SCALES_STEP = {1: 0, 2: 0, 3: 8}
 
 
 def tile_soft_hyperplane_hash_scores_k7_kernel(
@@ -74,7 +76,8 @@ def tile_soft_hyperplane_hash_scores_k7_kernel(
             return t[v, r0 : r0 + HALF, :].rearrange("(b r) k -> r b k", b=2)
 
         def load_x(h):
-            nc.sync.dma_start(out=x_sb[h][:], in_=rows(x, h))
+            r0 = (h % 2) * HALF
+            nc.sync.dma_start(out=x_sb[h][:], in_=x[h // 2, r0 : r0 + HALF, :].rearrange("(r b) k -> r b k", b=2))
 
         def load_lex(h):
             nc.sync.dma_start(out=lex_sb[h][:], in_=rows(lex, h))
@@ -103,29 +106,38 @@ def tile_soft_hyperplane_hash_scores_k7_kernel(
             )
         load_x(1)
         load_h(1)
-        load_x(2)
         load_plane(h_rest, h_scales[1:G])
+        load_x(2)
         load_plane(c_first, c_scales[0:2])
         load_c(0)
+        load_h(2)
         load_lex(0)
         load_x(3)
         load_lex(1)
+        load_x(4)
         load_plane(c_rest, c_scales[2 : 2 * G])
-        for v in range(1, G):
-            load_c(v)
-            if v + 1 < G:
-                load_h(v + 1)
-                load_x(2 * v + 2)
-            load_lex(2 * v)
-            if v + 1 < G:
-                load_x(2 * v + 3)
-            load_lex(2 * v + 1)
+        load_c(1)
+        load_lex(2)
+        load_x(5)
+        load_h(3)
+        load_lex(3)
+        load_x(6)
+        load_c(2)
+        load_lex(4)
+        load_x(7)
+        load_lex(5)
+        load_c(3)
+        load_lex(6)
+        load_lex(7)
 
         def turn_vecs():
             bank = next_bank()
             words = vec_rows[:].bitcast(F32)
             for u in range(2):
                 nc.tensor.transpose(bank[:, u * P : (u + 1) * P], words[:, u : 2 * P : 2], ident[:])
+            return bank
+
+        def copy_vecs(bank):
             turned = bank[:, 0 : 2 * P].bitcast(BF16).rearrange("p (u j e) -> p j u e", u=2, e=2)
             nc.scalar.copy(out=vecs[:].rearrange("p j (u e) -> p j u e", u=2), in_=turned[:, 0 : 3 * 2 * G])
 
@@ -144,8 +156,8 @@ def tile_soft_hyperplane_hash_scores_k7_kernel(
         def copy_x(h):
             t = work.tile([P, HALF * PACK], BF16, name="xg%d" % h, tag="xg", bufs=2, align_bytes=64)
             nc.scalar.copy(
-                out=t[:].bitcast(F32).rearrange("p (b r u) -> p b r u", b=2, u=2),
-                in_=x_bank[h][:].rearrange("p (b u r) -> p b r u", b=2, u=2),
+                out=t[:].bitcast(F32).rearrange("p (r b u) -> p r b u", b=2, u=2),
+                in_=x_bank[h][:].rearrange("p (b u r) -> p r b u", b=2, u=2),
             )
             x_grouped[h] = t
 
@@ -239,8 +251,7 @@ def tile_soft_hyperplane_hash_scores_k7_kernel(
             h, dh = divmod(s, 2)
             if b == 0:
                 sum_sb[s] = work.tile([P, 2, KP], F32, name="sum%d" % s, tag="sum")
-            t = sum_sb[s]
-            for t in (t,):
+            for t in (sum_sb[s],):
                 nc.vector.tensor_tensor(
                     out=t[:, b, :].rearrange("r (t c i) -> r c t i", t=PACK, i=4),
                     in0=s_bank[s, b][:].rearrange("r (c i t) -> r c t i", t=PACK, i=4),
@@ -261,7 +272,7 @@ def tile_soft_hyperplane_hash_scores_k7_kernel(
         def finish(s):
             h, dh = divmod(s, 2)
             n = 2 * (h // 2) + dh
-            y = work.tile([P, PACK, HALF], F32, name="yt%d" % s, tag="yt")
+            y = work.tile([P, PACK, HALF], F32, name="yt%d" % s, tag="yt", bufs=4)
             for t in range(PACK):
                 u, e = divmod(t, 2)
                 src = t_bank[s, u][:, e * HALF : (e + 1) * HALF]
@@ -285,7 +296,8 @@ def tile_soft_hyperplane_hash_scores_k7_kernel(
             h, dh = divmod(s, 2)
             for b in range(2):
                 y = work.tile([P, KP], F32, name="y%d_%d" % (s, b), tag="y", bufs=4)
-                nc.scalar.copy(
+                copy = nc.vector.tensor_copy if (s, b) == (STEPS - 1, 1) else nc.scalar.copy
+                copy(
                     out=y[:].rearrange("r (p t) -> r p t", t=PACK),
                     in_=b_bank[s, b][:].rearrange("r (t p) -> r p t", t=PACK),
                 )
@@ -293,7 +305,7 @@ def tile_soft_hyperplane_hash_scores_k7_kernel(
                 nc.sync.dma_start(out=out_0[h // 2, r0 : r0 + P, KP * dh : KP * (dh + 1)], in_=y[:])
 
         def group_y(s):
-            t = work.tile([P, HALF * PACK], BF16, name="yb%d" % s, tag="yb", bufs=2, align_bytes=64)
+            t = work.tile([P, HALF * PACK], BF16, name="yb%d" % s, tag="yb", bufs=3, align_bytes=64)
             copy = nc.scalar.copy if s in GROUP_ON_SCALAR else nc.vector.tensor_copy
             copy(
                 out=t[:].rearrange("p (c i t) -> p c t i", t=PACK, i=4),
@@ -327,16 +339,17 @@ def tile_soft_hyperplane_hash_scores_k7_kernel(
             return max(0, project_step(first) - lead) == step
 
         turn_x(0)
+        vec_bank = turn_vecs()
         permute_words(0, 0, P)
-        turn_vecs()
         copy_x(0)
+        copy_vecs(vec_bank)
         permute_scales(0, 0, P)
         quantize_x(0)
         permute_words(0, P, 2 * P)
         permute_scales(0, P, 2 * P)
 
         for step in range(STEPS + LAG_B):
-            s_s, s_t, s_b = step - LAG_S, step - LAG_T, step - LAG_B
+            s_s, s_t, s_g, s_b = step - LAG_S, step - LAG_T, step - LAG_G, step - LAG_B
             projected = [s for s in range(STEPS) if project_step(s) == step]
             turned = [h for h in range(1, HALVES) if due(2 * h, 2, step)]
             if live(s_s):
@@ -349,27 +362,26 @@ def tile_soft_hyperplane_hash_scores_k7_kernel(
                 turn_sum(s_t)
             if live(s_b):
                 turn_back(s_b)
-            if live(s_b) and s_b in GROUP_ON_SCALAR:
-                group_y(s_b)
             for s in projected:
                 soften(s)
             for h in turned:
                 copy_x(h)
-            if live(s_s):
-                add_lex(s_s, 0)
             if live(step - 1) and step % 2 == 0:
                 quantize_z(step // 2 - 1)
-            if live(s_b) and s_b not in GROUP_ON_SCALAR:
-                group_y(s_b)
+            if live(s_s):
+                add_lex(s_s, 0)
+            if live(s_g) and s_g not in GROUP_ON_SCALAR:
+                group_y(s_g)
             if live(s_s):
                 add_lex(s_s, 1)
             for h in range(1, HALVES):
                 if due(2 * h, 1, step):
                     quantize_x(h)
             for v in range(1, G):
-                if due(4 * v, 2, step):
+                if WORDS_STEP[v] == step:
                     permute_words(v, 0, 2 * P)
-                if due(4 * v, 1, step):
+            for v in range(1, G):
+                if SCALES_STEP[v] == step:
                     permute_scales(v, 0, 2 * P)
             if live(step):
                 apply_gain(step)
@@ -378,3 +390,5 @@ def tile_soft_hyperplane_hash_scores_k7_kernel(
             if live(s_b):
                 quantize_y(s_b)
                 store_y(s_b)
+            if live(s_g) and s_g in GROUP_ON_SCALAR:
+                group_y(s_g)

@@ -22,11 +22,10 @@ KP = P * PACK
 HALF = 256
 HALVES = G * R // HALF
 STEPS = 2 * HALVES
-BANKS = 8
-LAG_S, LAG_T, LAG_G, LAG_B = 3, 4, 5, 6
-GROUP_ON_SCALAR = (0,)
-WORDS_STEP = {1: 0, 2: 5, 3: 9}
-SCALES_STEP = {1: 0, 2: 0, 3: 8}
+BANKS = 7
+LAG_S, LAG_T, LAG_B, LAG_Q = 3, 4, 5, 6
+WORDS_STEP = {1: 0, 2: 6, 3: 10}
+SCALES_STEP = {1: 0, 2: 5, 3: 8}
 
 
 def tile_soft_hyperplane_hash_scores_k7_kernel(
@@ -67,8 +66,8 @@ def tile_soft_hyperplane_hash_scores_k7_kernel(
         lex_sb = [keep.tile([P, 2, D], BF16, name="lex%d" % h) for h in range(HALVES)]
         h_sb = [keep.tile([P, 2 * B], U8, name="h%d" % v) for v in range(G)]
         c_sb = [keep.tile([P, 2, 2 * D], U8, name="c%d" % v, align_bytes=64) for v in range(G)]
-        vecs = keep.tile([P, 3 * 2 * G, PACK], F32, name="vecs")
-        gain, dgain, dbias = [vecs[:, 2 * G * n : 2 * G * (n + 1), :] for n in range(3)]
+        vecs = keep.tile([P, 2 * 2 * G, PACK], F32, name="vecs")
+        dgain, dbias = [vecs[:, 2 * G * n : 2 * G * (n + 1), :] for n in range(2)]
         y_scales = keep.tile([P, 2, G * R], U8, name="y_scales", align_bytes=64)
 
         def rows(t, h):
@@ -130,8 +129,11 @@ def tile_soft_hyperplane_hash_scores_k7_kernel(
         load_lex(6)
         load_lex(7)
 
+        vec_bank = psum.tile([P, KP], F32, name="vec_bank")
+        vecs_turned = vec_bank[:, 0 : 2 * P].bitcast(BF16).rearrange("p (u j e) -> p j u e", u=2, e=2)
+
         def turn_vecs():
-            bank = next_bank()
+            bank = vec_bank
             words = vec_rows[:].bitcast(F32)
             for u in range(2):
                 nc.tensor.transpose(bank[:, u * P : (u + 1) * P], words[:, u : 2 * P : 2], ident[:])
@@ -139,7 +141,7 @@ def tile_soft_hyperplane_hash_scores_k7_kernel(
 
         def copy_vecs(bank):
             turned = bank[:, 0 : 2 * P].bitcast(BF16).rearrange("p (u j e) -> p j u e", u=2, e=2)
-            nc.scalar.copy(out=vecs[:].rearrange("p j (u e) -> p j u e", u=2), in_=turned[:, 0 : 3 * 2 * G])
+            nc.scalar.copy(out=vecs[:].rearrange("p j (u e) -> p j u e", u=2), in_=turned[:, 2 * G : 3 * 2 * G])
 
         x_bank, x_grouped, x_q, h_perm, p_bank, tanh_sb, z_bf, z_q = {}, {}, {}, {}, {}, {}, {}, {}
         s_bank, sum_sb, t_bank, y_t, b_bank, y_bf = {}, {}, {}, {}, {}, {}
@@ -217,7 +219,7 @@ def tile_soft_hyperplane_hash_scores_k7_kernel(
             if g == 0:
                 z_bf[h] = work.tile([P, 2 * HALF * PACK], BF16, name="z%d" % h, tag="z", bufs=2, align_bytes=64)
             t = z_bf[h][:, g * HALF * PACK : (g + 1) * HALF * PACK]
-            factor = gain[:, 2 * (h // 2) + g, :].rearrange("p (u e) -> p u e", u=2)
+            factor = vecs_turned[:, 2 * (h // 2) + g]
             nc.vector.tensor_tensor(
                 out=t.rearrange("p (r u e) -> p r u e", u=2, e=2),
                 in0=tanh_sb[s][:].rearrange("p u r e -> p r u e"),
@@ -296,7 +298,7 @@ def tile_soft_hyperplane_hash_scores_k7_kernel(
             h, dh = divmod(s, 2)
             for b in range(2):
                 y = work.tile([P, KP], F32, name="y%d_%d" % (s, b), tag="y", bufs=4)
-                copy = nc.vector.tensor_copy if (s, b) == (STEPS - 1, 1) else nc.scalar.copy
+                copy = nc.vector.tensor_copy if b == 1 and s % 3 == 2 else nc.scalar.copy
                 copy(
                     out=y[:].rearrange("r (p t) -> r p t", t=PACK),
                     in_=b_bank[s, b][:].rearrange("r (t p) -> r p t", t=PACK),
@@ -306,11 +308,20 @@ def tile_soft_hyperplane_hash_scores_k7_kernel(
 
         def group_y(s):
             t = work.tile([P, HALF * PACK], BF16, name="yb%d" % s, tag="yb", bufs=3, align_bytes=64)
-            copy = nc.scalar.copy if s in GROUP_ON_SCALAR else nc.vector.tensor_copy
-            copy(
-                out=t[:].rearrange("p (c i t) -> p c t i", t=PACK, i=4),
-                in_=y_t[s][:].rearrange("p t (c i) -> p c t i", i=4),
-            )
+            if s < STEPS - 2:
+                nc.gpsimd.tensor_scalar(
+                    out=t[:].rearrange("p (r t) -> p r t", t=PACK),
+                    in0=y_t[s][:].rearrange("p t r -> p r t"),
+                    scalar1=1.0,
+                    scalar2=-0.0,
+                    op0=ALU.mult,
+                    op1=ALU.add,
+                )
+            else:
+                nc.vector.tensor_copy(
+                    out=t[:].rearrange("p (c i t) -> p c t i", t=PACK, i=4),
+                    in_=y_t[s][:].rearrange("p t (c i) -> p c t i", i=4),
+                )
             y_bf[s] = t
 
         def quantize_y(s):
@@ -339,7 +350,7 @@ def tile_soft_hyperplane_hash_scores_k7_kernel(
             return max(0, project_step(first) - lead) == step
 
         turn_x(0)
-        vec_bank = turn_vecs()
+        turn_vecs()
         permute_words(0, 0, P)
         copy_x(0)
         copy_vecs(vec_bank)
@@ -348,8 +359,8 @@ def tile_soft_hyperplane_hash_scores_k7_kernel(
         permute_words(0, P, 2 * P)
         permute_scales(0, P, 2 * P)
 
-        for step in range(STEPS + LAG_B):
-            s_s, s_t, s_g, s_b = step - LAG_S, step - LAG_T, step - LAG_G, step - LAG_B
+        for step in range(STEPS + LAG_Q):
+            s_s, s_t, s_b, s_q = step - LAG_S, step - LAG_T, step - LAG_B, step - LAG_Q
             projected = [s for s in range(STEPS) if project_step(s) == step]
             turned = [h for h in range(1, HALVES) if due(2 * h, 2, step)]
             if live(s_s):
@@ -370,10 +381,11 @@ def tile_soft_hyperplane_hash_scores_k7_kernel(
                 quantize_z(step // 2 - 1)
             if live(s_s):
                 add_lex(s_s, 0)
-            if live(s_g) and s_g not in GROUP_ON_SCALAR:
-                group_y(s_g)
-            if live(s_s):
                 add_lex(s_s, 1)
+            if live(step) and step >= LAG_B:
+                apply_gain(step)
+            if live(s_b):
+                group_y(s_b)
             for h in range(1, HALVES):
                 if due(2 * h, 1, step):
                     quantize_x(h)
@@ -383,12 +395,11 @@ def tile_soft_hyperplane_hash_scores_k7_kernel(
             for v in range(1, G):
                 if SCALES_STEP[v] == step:
                     permute_scales(v, 0, 2 * P)
-            if live(step):
+            if step < LAG_B:
                 apply_gain(step)
             if live(s_t):
                 finish(s_t)
+            if live(s_q):
+                quantize_y(s_q)
             if live(s_b):
-                quantize_y(s_b)
                 store_y(s_b)
-            if live(s_g) and s_g in GROUP_ON_SCALAR:
-                group_y(s_g)

@@ -18,14 +18,20 @@ ALU = mybir.AluOpType
 
 P = 128
 PACK = 4
-KP = P * PACK
+GROUP = P * PACK
+QUADRANTS = 4
 HALF = 256
 HALVES = G * R // HALF
 STEPS = 2 * HALVES
-BANKS = 7
-LAG_S, LAG_T, LAG_B, LAG_Q = 3, 4, 5, 6
-WORDS_STEP = {1: 0, 2: 6, 3: 10}
-SCALES_STEP = {1: 0, 2: 5, 3: 8}
+VEC_ROWS = 2 * G
+ROTATING_BANKS = 7
+LINE = 4
+
+LAG_SCORE, LAG_FINISH, LAG_BACK, LAG_PLANES = 3, 4, 5, 6
+FIRST_LEADING_STEP = 3
+REORDER_ROUND = {1: 0, 2: 5, 3: 9}
+VECTOR_COPY_PERIOD = 3
+TAIL_STEPS = 2
 
 
 def tile_soft_hyperplane_hash_scores_k7_kernel(
@@ -43,43 +49,48 @@ def tile_soft_hyperplane_hash_scores_k7_kernel(
         def next_bank():
             n = len(bank_uses)
             bank_uses.append(n)
-            return psum.tile([P, KP], F32, name="bank%d" % n, tag="bank%d" % (n % BANKS))
+            return psum.tile([P, GROUP], F32, name="bank%d" % n, tag="bank%d" % (n % ROTATING_BANKS))
 
-        vec_rows = keep.tile([P, KP], BF16, name="vec_rows")
+        vec_rows = keep.tile([P, GROUP], BF16, name="vec_rows")
         nc.gpsimd.memset(vec_rows[:].bitcast(I32), 0)
         ident = keep.tile([P, P], F32, name="ident")
         make_identity(nc, ident[:])
 
-        warm = keep.tile([P, 1], F32, name="warm")
-        nc.scalar.activation(out=warm[:], in_=ident[:, 0:1], func=ACT.Tanh)
+        zero_bias = keep.tile([P, 1], F32, name="zero_bias")
+        nc.scalar.activation(out=zero_bias[:], in_=ident[:, 0:1], func=ACT.Tanh, scale=0.0)
 
-        h_first = keep.tile([P, 1, B], U8, name="h_first", align_bytes=64)
-        h_rest = keep.tile([P, G - 1, B], U8, name="h_rest", align_bytes=64)
+        h_packed = keep.tile([P, 1, B], U8, name="h_packed", align_bytes=64)
+        h_later = keep.tile([P, G - 1, B], U8, name="h_later", align_bytes=64)
         c_first = keep.tile([P, 2, D], U8, name="c_first", align_bytes=64)
-        c_rest = keep.tile([P, 2 * (G - 1), D], U8, name="c_rest", align_bytes=64)
-        for plane in (h_first, h_rest, c_first, c_rest):
+        c_later = keep.tile([P, 2 * (G - 1), D], U8, name="c_later", align_bytes=64)
+        for plane in (h_packed, h_later, c_first, c_later):
             nc.vector.memset(plane[:].rearrange("p v n -> p (v n)").bitcast(I32), 0)
-        h_plane = [h_first[:, 0, :]] + [h_rest[:, n, :] for n in range(G - 1)]
-        c_plane = [c_first[:, n, :] for n in range(2)] + [c_rest[:, n, :] for n in range(2 * (G - 1))]
+        c_plane = [c_first[:, n, :] for n in range(2)] + [c_later[:, n, :] for n in range(2 * (G - 1))]
 
         x_sb = [keep.tile([P, 2, K], BF16, name="x%d" % h) for h in range(HALVES)]
         lex_sb = [keep.tile([P, 2, D], BF16, name="lex%d" % h) for h in range(HALVES)]
         h_sb = [keep.tile([P, 2 * B], U8, name="h%d" % v) for v in range(G)]
         c_sb = [keep.tile([P, 2, 2 * D], U8, name="c%d" % v, align_bytes=64) for v in range(G)]
-        vecs = keep.tile([P, 2 * 2 * G, PACK], F32, name="vecs")
-        dgain, dbias = [vecs[:, 2 * G * n : 2 * G * (n + 1), :] for n in range(2)]
-        y_scales = keep.tile([P, 2, G * R], U8, name="y_scales", align_bytes=64)
+        doc_vecs = keep.tile([P, 2 * VEC_ROWS, PACK], F32, name="doc_vecs")
+        doc_gain_sb, doc_bias_sb = doc_vecs[:, 0:VEC_ROWS, :], doc_vecs[:, VEC_ROWS : 2 * VEC_ROWS, :]
+        y_plane = keep.tile([P, 2, G * R], U8, name="y_plane", align_bytes=64)
 
-        def rows(t, h):
-            v, r0 = h // 2, (h % 2) * HALF
-            return t[v, r0 : r0 + HALF, :].rearrange("(b r) k -> r b k", b=2)
+        h_ordered = [keep.tile([P, PACK, 2 * P, 2], U8, name="hw%d" % v, align_bytes=64) for v in range(G)]
+        packed_ordered = keep.tile([P, PACK, 2 * P], U8, name="packed_ordered", align_bytes=64)
+        h_plane = [packed_ordered] + [h_later[:, n, :].rearrange("p (t m) -> p t m", t=PACK) for n in range(G - 1)]
+
+        vec_bank = psum.tile([P, GROUP], F32, name="vec_bank")
+        vecs_turned = vec_bank[:, 0 : 2 * P].bitcast(BF16).rearrange("p (u j e) -> p j u e", u=2, e=2)
+
+        def half_rows(tensor, h):
+            r0 = (h % 2) * HALF
+            return tensor[h // 2, r0 : r0 + HALF, :]
 
         def load_x(h):
-            r0 = (h % 2) * HALF
-            nc.sync.dma_start(out=x_sb[h][:], in_=x[h // 2, r0 : r0 + HALF, :].rearrange("(r b) k -> r b k", b=2))
+            nc.sync.dma_start(out=x_sb[h][:], in_=half_rows(x, h).rearrange("(i b) k -> i b k", b=2))
 
         def load_lex(h):
-            nc.sync.dma_start(out=lex_sb[h][:], in_=rows(lex, h))
+            nc.sync.dma_start(out=lex_sb[h][:], in_=half_rows(lex, h).rearrange("(b r) d -> r b d", b=2))
 
         def load_h(v):
             nc.sync.dma_start(out=h_sb[v][:].bitcast(I32), in_=h_words[v].bitcast(I32))
@@ -89,32 +100,262 @@ def tile_soft_hyperplane_hash_scores_k7_kernel(
                 out=c_sb[v][:].bitcast(I32), in_=c_words[2 * v : 2 * v + 2].rearrange("g p n -> p g n").bitcast(I32)
             )
 
-        def load_plane(plane, scales):
-            for q in range(4):
+        def load_c_planes(planes, scales):
+            for q in range(QUADRANTS):
                 nc.sync.dma_start(
-                    out=plane[32 * q : 32 * q + 4].bitcast(I32),
+                    out=planes[32 * q : 32 * q + 4].bitcast(I32),
                     in_=scales[:, 4 * q : 4 * q + 4, :].rearrange("g r n -> r g n").bitcast(I32),
                 )
 
+        def load_h_packed():
+            for q in range(QUADRANTS):
+                nc.sync.dma_start(
+                    out=h_packed[32 * q : 32 * q + 4 * G, 0, :].bitcast(I32),
+                    in_=h_scales[:, 4 * q : 4 * q + 4, :].bitcast(I32),
+                )
+
+        def load_vecs():
+            for n, vec in enumerate((bit_gain, doc_gain, doc_bias)):
+                nc.sync.dma_start(
+                    out=vec_rows[VEC_ROWS * n : VEC_ROWS * (n + 1), :], in_=vec.rearrange("v (g k) -> (v g) k", g=2)
+                )
+
+        def spread_h_scales(v):
+            flat = packed_ordered[:].rearrange("p t m -> p (t m)")
+            for q in range(QUADRANTS):
+                nc.sync.dma_start(
+                    out=h_later[32 * q : 32 * q + 4, v - 1, :].bitcast(I32),
+                    in_=flat[32 * q + 4 * v : 32 * q + 4 * v + 4, :].bitcast(I32),
+                )
+
+        x_bank, x_grouped, x_mx, p_bank, tanh_sb, z_grouped, z_mx = {}, {}, {}, {}, {}, {}, {}
+        s_bank, sum_sb, sum_bank, y_turned, y_bank, y_grouped = {}, {}, {}, {}, {}, {}
+
+        def turn_pairs(bank, first_slot, rows):
+            words = rows.bitcast(F32)
+            for u in range(2):
+                slot = first_slot + u
+                nc.tensor.transpose(bank[:, slot * P : (slot + 1) * P], words[:, u : 2 * P : 2], ident[:])
+
+        def copy_doc_vecs():
+            nc.scalar.copy(
+                out=doc_vecs[:].rearrange("p j (u e) -> p j u e", u=2), in_=vecs_turned[:, VEC_ROWS : 3 * VEC_ROWS]
+            )
+
+        def turn_x(h):
+            x_bank[h] = next_bank()
+            for b in range(2):
+                turn_pairs(x_bank[h], 2 * b, x_sb[h][:, b, :])
+
+        def group_x(h):
+            x_grouped[h] = work.tile([P, HALF * PACK], BF16, name="xg%d" % h, tag="xg", bufs=2, align_bytes=64)
+            nc.scalar.copy(
+                out=x_grouped[h][:].bitcast(F32).rearrange("p (i b u) -> p i b u", b=2, u=2),
+                in_=x_bank[h][:].rearrange("p (b u i) -> p i b u", b=2, u=2),
+            )
+
+        def quantize(src, width, tag, n):
+            codes = work.tile([P, width], U32, name="%s_codes%d" % (tag, n), tag=tag + "_codes", align_bytes=64)
+            plane = work.tile([P, width], U8, name="%s_plane%d" % (tag, n), tag=tag + "_plane", align_bytes=64)
+            nc.vector.quantize_mx(out=codes[:].bitcast(FP8X4), scales=plane[:], in_=src[:])
+            return codes, plane
+
+        def quantize_x(h):
+            x_mx[h] = quantize(x_grouped[h], HALF, "x", h)
+
+        def reorder_h_words(v, g):
+            cols = slice(g * P, (g + 1) * P)
+            nc.vector.tensor_copy(
+                out=h_ordered[v][:, :, cols, :],
+                in_=h_sb[v][:].rearrange("p (m t b) -> p t m b", t=PACK, b=2)[:, :, cols, :],
+            )
+
+        def reorder_h_scales(g):
+            cols = slice(g * P, (g + 1) * P)
+            nc.vector.tensor_copy(
+                out=packed_ordered[:, :, cols], in_=h_packed[:, 0, :].rearrange("p (m t) -> p t m", t=PACK)[:, :, cols]
+            )
+
+        def project(s):
+            h, g = divmod(s, 2)
+            words = h_ordered[h // 2][:].rearrange("p t m b -> p t (m b)")
+            codes, plane = x_mx[h]
+            for u in range(2):
+                p_bank[s, u] = next_bank()
+                for e in range(2):
+                    t = 2 * u + e
+                    nc.tensor.matmul_mx(
+                        out=p_bank[s, u][:, e * HALF : (e + 1) * HALF],
+                        lhsT=words[:, t, 2 * P * g : 2 * P * (g + 1)].bitcast(FP4X4),
+                        lhsT_scale=h_plane[h // 2][:, t, P * g : P * (g + 1)],
+                        rhs=codes[:].bitcast(FP8X4),
+                        rhs_scale=plane[:],
+                        start=True,
+                        stop=True,
+                    )
+
+        def soften(s):
+            tanh_sb[s] = work.tile([P, 2, HALF, 2], F32, name="tanh%d" % s, tag="tanh", bufs=4)
+            for u in range(2):
+                nc.scalar.activation(
+                    out=tanh_sb[s][:, u],
+                    in_=p_bank[s, u][:].rearrange("p (e r) -> p r e", e=2),
+                    func=ACT.Tanh,
+                    bias=zero_bias[:],
+                )
+
+        def apply_gain(s):
+            h, g = divmod(s, 2)
+            if g == 0:
+                z_grouped[h] = work.tile([P, 2 * HALF * PACK], BF16, name="z%d" % h, tag="z", bufs=2, align_bytes=64)
+            z = z_grouped[h][:, g * HALF * PACK : (g + 1) * HALF * PACK]
+            nc.vector.tensor_tensor(
+                out=z.rearrange("p (r u e) -> p r u e", u=2, e=2),
+                in0=tanh_sb[s][:].rearrange("p u r e -> p r u e"),
+                in1=vecs_turned[:, 2 * (h // 2) + g].unsqueeze(1).to_broadcast([P, HALF, 2, 2]),
+                op=ALU.mult,
+            )
+
+        def quantize_z(h):
+            z_mx[h] = quantize(z_grouped[h], 2 * HALF, "z", h)
+
+        def score(s):
+            h, dg = divmod(s, 2)
+            v = h // 2
+            codes, plane = z_mx[h]
+            for b in range(2):
+                s_bank[s, b] = next_bank()
+                for g in range(2):
+                    cols = slice(g * HALF + b * P, g * HALF + (b + 1) * P)
+                    nc.tensor.matmul_mx(
+                        out=s_bank[s, b][:],
+                        lhsT=codes[:, cols].bitcast(FP8X4),
+                        lhsT_scale=plane[:, cols],
+                        rhs=c_sb[v][:, g, 2 * GROUP * dg : 2 * GROUP * (dg + 1)].bitcast(FP4X4),
+                        rhs_scale=c_plane[2 * v + g][:, GROUP * dg : GROUP * (dg + 1)],
+                        start=(g == 0),
+                        stop=(g == 1),
+                    )
+
+        def add_lex(s):
+            h, dg = divmod(s, 2)
+            sum_sb[s] = work.tile([P, 2, GROUP], F32, name="sum%d" % s, tag="sum")
+            for b in range(2):
+                docs = lex_sb[h][:, b, GROUP * dg : GROUP * (dg + 1)]
+                nc.vector.tensor_tensor(
+                    out=sum_sb[s][:, b, :].rearrange("r (t c i) -> r c t i", t=PACK, i=LINE),
+                    in0=s_bank[s, b][:].rearrange("r (c i t) -> r c t i", t=PACK, i=LINE),
+                    in1=docs.rearrange("r (c i t) -> r c t i", t=PACK, i=LINE),
+                    op=ALU.add,
+                )
+
+        def turn_sum(s):
+            for u in range(2):
+                sum_bank[s, u] = next_bank()
+                for e in range(2):
+                    t = 2 * u + e
+                    for b in range(2):
+                        slot = 2 * e + b
+                        nc.tensor.transpose(
+                            sum_bank[s, u][:, slot * P : (slot + 1) * P], sum_sb[s][:, b, t * P : (t + 1) * P], ident[:]
+                        )
+
+        def finish(s):
+            h, dg = divmod(s, 2)
+            row = 2 * (h // 2) + dg
+            y_turned[s] = work.tile([P, PACK, HALF], F32, name="yt%d" % s, tag="yt", bufs=4)
+            for t in range(PACK):
+                u, e = divmod(t, 2)
+                dst, src = y_turned[s][:, t, :], sum_bank[s, u][:, e * HALF : (e + 1) * HALF]
+                gain, bias = doc_gain_sb[:, row, t : t + 1], doc_bias_sb[:, row, t : t + 1]
+                if u == 1 and s >= STEPS - TAIL_STEPS:
+                    nc.vector.tensor_scalar(out=dst, in0=src, scalar1=gain, scalar2=bias, op0=ALU.mult, op1=ALU.add)
+                else:
+                    nc.scalar.activation(out=dst, in_=src, func=ACT.Identity, scale=gain, bias=bias)
+
+        def turn_back(s):
+            for b in range(2):
+                y_bank[s, b] = next_bank()
+                for t in range(PACK):
+                    nc.tensor.transpose(
+                        y_bank[s, b][:, t * P : (t + 1) * P], y_turned[s][:, t, b * P : (b + 1) * P], ident[:]
+                    )
+
+        def store_y(s):
+            h, dg = divmod(s, 2)
+            for b in range(2):
+                y = work.tile([P, GROUP], F32, name="y%d_%d" % (s, b), tag="y", bufs=4)
+                on_vector = b == 1 and s % VECTOR_COPY_PERIOD == VECTOR_COPY_PERIOD - 1
+                copy = nc.vector.tensor_copy if on_vector else nc.scalar.copy
+                copy(
+                    out=y[:].rearrange("r (p t) -> r p t", t=PACK),
+                    in_=y_bank[s, b][:].rearrange("r (t p) -> r p t", t=PACK),
+                )
+                dst = half_rows(out_0, h)[b * P : (b + 1) * P, GROUP * dg : GROUP * (dg + 1)]
+                nc.sync.dma_start(out=dst, in_=y[:])
+
+        def group_y(s):
+            y_grouped[s] = work.tile([P, HALF * PACK], BF16, name="yg%d" % s, tag="yg", align_bytes=64)
+            if s < STEPS - TAIL_STEPS:
+                nc.gpsimd.tensor_scalar(
+                    out=y_grouped[s][:].rearrange("p (r t) -> p r t", t=PACK),
+                    in0=y_turned[s][:].rearrange("p t r -> p r t"),
+                    scalar1=1.0,
+                    scalar2=-0.0,
+                    op0=ALU.mult,
+                    op1=ALU.add,
+                )
+            else:
+                nc.vector.tensor_copy(
+                    out=y_grouped[s][:].rearrange("p (c i t) -> p c t i", t=PACK, i=LINE),
+                    in_=y_turned[s][:].rearrange("p t (c i) -> p c t i", i=LINE),
+                )
+
+        def store_planes(s):
+            h, dg = divmod(s, 2)
+            cols = slice(h * HALF, (h + 1) * HALF)
+            codes = work.tile([P, HALF], U32, name="y_codes%d" % s, tag="y_codes", align_bytes=64)
+            nc.vector.quantize_mx(out=codes[:].bitcast(FP8X4), scales=y_plane[:, dg, cols], in_=y_grouped[s][:])
+            nc.sync.dma_start(
+                out=out_1[dg, :, cols, :].rearrange("p m t -> p (m t)").bitcast(I32), in_=codes[:].bitcast(I32)
+            )
+            if (s + 1) % (STEPS // G) == 0:
+                view = slice((h // 2) * R, (h // 2 + 1) * R)
+                for q in range(QUADRANTS):
+                    nc.sync.dma_start(
+                        out=out_2[:, 4 * q : 4 * q + 4, view].rearrange("g r m -> r g m").bitcast(I32),
+                        in_=y_plane[32 * q : 32 * q + 4, :, view].bitcast(I32),
+                    )
+
         load_x(0)
         load_h(0)
-        load_plane(h_first, h_scales[0:1])
-        for n, vec in enumerate((bit_gain, doc_gain, doc_bias)):
-            nc.sync.dma_start(
-                out=vec_rows[2 * G * n : 2 * G * (n + 1), :], in_=vec.rearrange("v (g k) -> (v g) k", g=2)
-            )
+        load_h_packed()
+        load_vecs()
         load_x(1)
         load_h(1)
-        load_plane(h_rest, h_scales[1:G])
         load_x(2)
-        load_plane(c_first, c_scales[0:2])
+        load_c_planes(c_first, c_scales[0:2])
         load_c(0)
-        load_h(2)
         load_lex(0)
+
+        turn_x(0)
+        turn_pairs(vec_bank, 0, vec_rows[:])
+        reorder_h_words(0, 0)
+        group_x(0)
+        copy_doc_vecs()
+        reorder_h_scales(0)
+        quantize_x(0)
+        reorder_h_words(0, 1)
+        reorder_h_scales(1)
+
+        spread_h_scales(1)
+        load_h(2)
         load_x(3)
         load_lex(1)
         load_x(4)
-        load_plane(c_rest, c_scales[2 : 2 * G])
+        spread_h_scales(2)
+        spread_h_scales(3)
+        load_c_planes(c_later, c_scales[2 : 2 * G])
         load_c(1)
         load_lex(2)
         load_x(5)
@@ -129,277 +370,52 @@ def tile_soft_hyperplane_hash_scores_k7_kernel(
         load_lex(6)
         load_lex(7)
 
-        vec_bank = psum.tile([P, KP], F32, name="vec_bank")
-        vecs_turned = vec_bank[:, 0 : 2 * P].bitcast(BF16).rearrange("p (u j e) -> p j u e", u=2, e=2)
-
-        def turn_vecs():
-            bank = vec_bank
-            words = vec_rows[:].bitcast(F32)
-            for u in range(2):
-                nc.tensor.transpose(bank[:, u * P : (u + 1) * P], words[:, u : 2 * P : 2], ident[:])
-            return bank
-
-        def copy_vecs(bank):
-            turned = bank[:, 0 : 2 * P].bitcast(BF16).rearrange("p (u j e) -> p j u e", u=2, e=2)
-            nc.scalar.copy(out=vecs[:].rearrange("p j (u e) -> p j u e", u=2), in_=turned[:, 2 * G : 3 * 2 * G])
-
-        x_bank, x_grouped, x_q, h_perm, p_bank, tanh_sb, z_bf, z_q = {}, {}, {}, {}, {}, {}, {}, {}
-        s_bank, sum_sb, t_bank, y_t, b_bank, y_bf = {}, {}, {}, {}, {}, {}
-
-        def turn_x(h):
-            bank = next_bank()
-            for b in range(2):
-                words = x_sb[h][:, b, :].bitcast(F32)
-                for u in range(2):
-                    j = 2 * b + u
-                    nc.tensor.transpose(bank[:, j * P : (j + 1) * P], words[:, u : 2 * P : 2], ident[:])
-            x_bank[h] = bank
-
-        def copy_x(h):
-            t = work.tile([P, HALF * PACK], BF16, name="xg%d" % h, tag="xg", bufs=2, align_bytes=64)
-            nc.scalar.copy(
-                out=t[:].bitcast(F32).rearrange("p (r b u) -> p r b u", b=2, u=2),
-                in_=x_bank[h][:].rearrange("p (b u r) -> p r b u", b=2, u=2),
-            )
-            x_grouped[h] = t
-
-        def quantize(src, width, tag, n, bufs):
-            codes = work.tile([P, width], U32, name="%s_q%d" % (tag, n), tag=tag + "_q", bufs=bufs, align_bytes=64)
-            scales = work.tile([P, width], U8, name="%s_s%d" % (tag, n), tag=tag + "_s", bufs=bufs, align_bytes=64)
-            nc.vector.quantize_mx(out=codes[:].bitcast(FP8X4), scales=scales[:], in_=src[:])
-            return codes, scales
-
-        def quantize_x(h):
-            x_q[h] = quantize(x_grouped[h], HALF, "x", h, 3)
-
-        h_words_perm = [keep.tile([P, PACK, 2 * P, 2], U8, name="hw%d" % v, align_bytes=64) for v in range(G)]
-        h_scales_perm = [keep.tile([P, PACK, 2 * P], U8, name="hs%d" % v, align_bytes=64) for v in range(G)]
-
-        def permute_words(v, m0, m1):
-            nc.vector.tensor_copy(
-                out=h_words_perm[v][:, :, m0:m1, :],
-                in_=h_sb[v][:].rearrange("p (m t b) -> p t m b", t=PACK, b=2)[:, :, m0:m1, :],
-            )
-
-        def permute_scales(v, m0, m1):
-            nc.vector.tensor_copy(
-                out=h_scales_perm[v][:, :, m0:m1], in_=h_plane[v].rearrange("p (m t) -> p t m", t=PACK)[:, :, m0:m1]
-            )
-
-        def project(s):
-            h, g = divmod(s, 2)
-            words = h_words_perm[h // 2][:].rearrange("p t m b -> p t (m b)")
-            scales = h_scales_perm[h // 2]
-            codes, code_scales = x_q[h]
-            for u in range(2):
-                bank = next_bank()
-                for e in range(2):
-                    t = 2 * u + e
-                    nc.tensor.matmul_mx(
-                        out=bank[:, e * HALF : (e + 1) * HALF],
-                        lhsT=words[:, t, 2 * P * g : 2 * P * (g + 1)].bitcast(FP4X4),
-                        lhsT_scale=scales[:, t, P * g : P * (g + 1)],
-                        rhs=codes[:].bitcast(FP8X4),
-                        rhs_scale=code_scales[:],
-                        start=True,
-                        stop=True,
-                    )
-                p_bank[s, u] = bank
-
-        def soften(s):
-            t = work.tile([P, 2, HALF, 2], F32, name="tanh%d" % s, tag="tanh", bufs=4)
-            for u in range(2):
-                nc.scalar.activation(
-                    out=t[:, u], in_=p_bank[s, u][:].rearrange("p (e r) -> p r e", e=2), func=ACT.Tanh
-                )
-            tanh_sb[s] = t
-
-        def apply_gain(s):
-            h, g = divmod(s, 2)
-            if g == 0:
-                z_bf[h] = work.tile([P, 2 * HALF * PACK], BF16, name="z%d" % h, tag="z", bufs=2, align_bytes=64)
-            t = z_bf[h][:, g * HALF * PACK : (g + 1) * HALF * PACK]
-            factor = vecs_turned[:, 2 * (h // 2) + g]
-            nc.vector.tensor_tensor(
-                out=t.rearrange("p (r u e) -> p r u e", u=2, e=2),
-                in0=tanh_sb[s][:].rearrange("p u r e -> p r u e"),
-                in1=factor.unsqueeze(1).to_broadcast([P, HALF, 2, 2]),
-                op=ALU.mult,
-            )
-
-        def quantize_z(h):
-            z_q[h] = quantize(z_bf[h], 2 * HALF, "z", h, 3)
-
-        def score(s):
-            h, dh = divmod(s, 2)
-            v = h // 2
-            for b in range(2):
-                bank = next_bank()
-                for g in range(2):
-                    codes, scales = z_q[h]
-                    cols = slice(g * HALF + b * P, g * HALF + (b + 1) * P)
-                    nc.tensor.matmul_mx(
-                        out=bank[:],
-                        lhsT=codes[:, cols].bitcast(FP8X4),
-                        lhsT_scale=scales[:, cols],
-                        rhs=c_sb[v][:, g, 2 * KP * dh : 2 * KP * (dh + 1)].bitcast(FP4X4),
-                        rhs_scale=c_plane[2 * v + g][:, KP * dh : KP * (dh + 1)],
-                        start=(g == 0),
-                        stop=(g == 1),
-                    )
-                s_bank[s, b] = bank
-
-        def add_lex(s, b):
-            h, dh = divmod(s, 2)
-            if b == 0:
-                sum_sb[s] = work.tile([P, 2, KP], F32, name="sum%d" % s, tag="sum")
-            for t in (sum_sb[s],):
-                nc.vector.tensor_tensor(
-                    out=t[:, b, :].rearrange("r (t c i) -> r c t i", t=PACK, i=4),
-                    in0=s_bank[s, b][:].rearrange("r (c i t) -> r c t i", t=PACK, i=4),
-                    in1=lex_sb[h][:, b, KP * dh : KP * (dh + 1)].rearrange("r (c i t) -> r c t i", t=PACK, i=4),
-                    op=ALU.add,
-                )
-
-        def turn_sum(s):
-            for u in range(2):
-                bank = next_bank()
-                for e in range(2):
-                    t = 2 * u + e
-                    for b in range(2):
-                        j = 2 * e + b
-                        nc.tensor.transpose(bank[:, j * P : (j + 1) * P], sum_sb[s][:, b, t * P : (t + 1) * P], ident[:])
-                t_bank[s, u] = bank
-
-        def finish(s):
-            h, dh = divmod(s, 2)
-            n = 2 * (h // 2) + dh
-            y = work.tile([P, PACK, HALF], F32, name="yt%d" % s, tag="yt", bufs=4)
-            for t in range(PACK):
-                u, e = divmod(t, 2)
-                src = t_bank[s, u][:, e * HALF : (e + 1) * HALF]
-                scale, bias = dgain[:, n, t : t + 1], dbias[:, n, t : t + 1]
-                if u == 1 and s >= STEPS - 2:
-                    nc.vector.tensor_scalar(
-                        out=y[:, t, :], in0=src, scalar1=scale, scalar2=bias, op0=ALU.mult, op1=ALU.add
-                    )
-                else:
-                    nc.scalar.activation(out=y[:, t, :], in_=src, func=ACT.Identity, scale=scale, bias=bias)
-            y_t[s] = y
-
-        def turn_back(s):
-            for b in range(2):
-                bank = next_bank()
-                for t in range(PACK):
-                    nc.tensor.transpose(bank[:, t * P : (t + 1) * P], y_t[s][:, t, b * P : (b + 1) * P], ident[:])
-                b_bank[s, b] = bank
-
-        def store_y(s):
-            h, dh = divmod(s, 2)
-            for b in range(2):
-                y = work.tile([P, KP], F32, name="y%d_%d" % (s, b), tag="y", bufs=4)
-                copy = nc.vector.tensor_copy if b == 1 and s % 3 == 2 else nc.scalar.copy
-                copy(
-                    out=y[:].rearrange("r (p t) -> r p t", t=PACK),
-                    in_=b_bank[s, b][:].rearrange("r (t p) -> r p t", t=PACK),
-                )
-                r0 = (h % 2) * HALF + b * P
-                nc.sync.dma_start(out=out_0[h // 2, r0 : r0 + P, KP * dh : KP * (dh + 1)], in_=y[:])
-
-        def group_y(s):
-            t = work.tile([P, HALF * PACK], BF16, name="yb%d" % s, tag="yb", bufs=3, align_bytes=64)
-            if s < STEPS - 2:
-                nc.gpsimd.tensor_scalar(
-                    out=t[:].rearrange("p (r t) -> p r t", t=PACK),
-                    in0=y_t[s][:].rearrange("p t r -> p r t"),
-                    scalar1=1.0,
-                    scalar2=-0.0,
-                    op0=ALU.mult,
-                    op1=ALU.add,
-                )
-            else:
-                nc.vector.tensor_copy(
-                    out=t[:].rearrange("p (c i t) -> p c t i", t=PACK, i=4),
-                    in_=y_t[s][:].rearrange("p t (c i) -> p c t i", i=4),
-                )
-            y_bf[s] = t
-
-        def quantize_y(s):
-            h, dh = divmod(s, 2)
-            cols = slice(h * HALF, (h + 1) * HALF)
-            codes = work.tile([P, HALF], U32, name="yq%d" % s, tag="yq", align_bytes=64)
-            nc.vector.quantize_mx(out=codes[:].bitcast(FP8X4), scales=y_scales[:, dh, cols], in_=y_bf[s][:])
-            nc.sync.dma_start(
-                out=out_1[dh, :, cols, :].rearrange("p m t -> p (m t)").bitcast(I32), in_=codes[:].bitcast(I32)
-            )
-            if s % 4 == 3:
-                view = slice((h // 2) * R, (h // 2 + 1) * R)
-                for q in range(4):
-                    nc.sync.dma_start(
-                        out=out_2[:, 4 * q : 4 * q + 4, view].rearrange("g r m -> r g m").bitcast(I32),
-                        in_=y_scales[32 * q : 32 * q + 4, :, view].bitcast(I32),
-                    )
-
         def live(s):
             return 0 <= s < STEPS
 
-        def project_step(s):
-            return s if s <= 2 else s - 1
+        def project_round(s):
+            return s if s < FIRST_LEADING_STEP else s - 1
 
-        def due(first, lead, step):
-            return max(0, project_step(first) - lead) == step
+        for n in range(STEPS + LAG_PLANES):
+            s_score, s_finish, s_back, s_planes = n - LAG_SCORE, n - LAG_FINISH, n - LAG_BACK, n - LAG_PLANES
+            projected = [s for s in range(STEPS) if project_round(s) == n]
+            turned = [h for h in range(1, HALVES) if project_round(2 * h) - 2 == n]
+            quantized = [h for h in range(1, HALVES) if project_round(2 * h) - 1 == n]
 
-        turn_x(0)
-        turn_vecs()
-        permute_words(0, 0, P)
-        copy_x(0)
-        copy_vecs(vec_bank)
-        permute_scales(0, 0, P)
-        quantize_x(0)
-        permute_words(0, P, 2 * P)
-        permute_scales(0, P, 2 * P)
-
-        for step in range(STEPS + LAG_Q):
-            s_s, s_t, s_b, s_q = step - LAG_S, step - LAG_T, step - LAG_B, step - LAG_Q
-            projected = [s for s in range(STEPS) if project_step(s) == step]
-            turned = [h for h in range(1, HALVES) if due(2 * h, 2, step)]
-            if live(s_s):
-                score(s_s)
+            if live(s_score):
+                score(s_score)
             for s in projected:
                 project(s)
             for h in turned:
                 turn_x(h)
-            if live(s_t):
-                turn_sum(s_t)
-            if live(s_b):
-                turn_back(s_b)
+            if live(s_finish):
+                turn_sum(s_finish)
+            if live(s_back):
+                turn_back(s_back)
+
             for s in projected:
                 soften(s)
             for h in turned:
-                copy_x(h)
-            if live(step - 1) and step % 2 == 0:
-                quantize_z(step // 2 - 1)
-            if live(s_s):
-                add_lex(s_s, 0)
-                add_lex(s_s, 1)
-            if live(step) and step >= LAG_B:
-                apply_gain(step)
-            if live(s_b):
-                group_y(s_b)
-            for h in range(1, HALVES):
-                if due(2 * h, 1, step):
-                    quantize_x(h)
+                group_x(h)
+            if live(n - 1) and n % 2 == 0:
+                quantize_z(n // 2 - 1)
+            if live(s_score):
+                add_lex(s_score)
+            if live(n) and n >= FIRST_LEADING_STEP:
+                apply_gain(n)
+            if live(s_back):
+                group_y(s_back)
+            for h in quantized:
+                quantize_x(h)
             for v in range(1, G):
-                if WORDS_STEP[v] == step:
-                    permute_words(v, 0, 2 * P)
-            for v in range(1, G):
-                if SCALES_STEP[v] == step:
-                    permute_scales(v, 0, 2 * P)
-            if step < LAG_B:
-                apply_gain(step)
-            if live(s_t):
-                finish(s_t)
-            if live(s_q):
-                quantize_y(s_q)
-            if live(s_b):
-                store_y(s_b)
+                for g in range(2):
+                    if REORDER_ROUND[v] + g == n:
+                        reorder_h_words(v, g)
+            if n < FIRST_LEADING_STEP:
+                apply_gain(n)
+            if live(s_finish):
+                finish(s_finish)
+            if live(s_planes):
+                store_planes(s_planes)
+            if live(s_back):
+                store_y(s_back)

from contextlib import ExitStack

import concourse.mybir as mybir
from concourse.masks import make_identity

G, R, K, B, D = 4, 512, 512, 1024, 1024
FLOPS = 2 * G * R * (K * B + B * D)

F32 = mybir.dt.float32
BF16 = mybir.dt.bfloat16
I32 = mybir.dt.int32
U32 = mybir.dt.uint32
U8 = mybir.dt.uint8
FP8X4 = mybir.dt.float8_e4m3fn_x4
FP4X4 = mybir.dt.float4_e2m1fn_x4
ACT = mybir.ActivationFunctionType
ALU = mybir.AluOpType

P = 128
PACK = 4
GROUP = P * PACK
QUADRANTS = 4
HALF = 256
HALVES = G * R // HALF
STEPS = 2 * HALVES
VEC_ROWS = 2 * G
ROTATING_BANKS = 7
LINE = 4

LAG_SCORE, LAG_FINISH, LAG_BACK, LAG_PLANES = 3, 4, 5, 6
FIRST_LEADING_STEP = 3
REORDER_ROUND = {1: 0, 2: 5, 3: 9}
VECTOR_COPY_PERIOD = 3
TAIL_STEPS = 2


def tile_soft_hyperplane_hash_scores_k7_kernel(
    tc, x, h_words, h_scales, bit_gain, c_words, c_scales, lex, doc_gain, doc_bias, out_0, out_1, out_2
):
    nc = tc.nc
    with ExitStack() as ctx:
        keep = ctx.enter_context(tc.tile_pool(name="keep", bufs=1))
        work = ctx.enter_context(tc.tile_pool(name="work", bufs=3))
        psum = ctx.enter_context(tc.psum_pool(name="psum", bufs=1))
        ctx.enter_context(tc.manual_schedule())

        bank_uses = []

        def next_bank():
            n = len(bank_uses)
            bank_uses.append(n)
            return psum.tile([P, GROUP], F32, name="bank%d" % n, tag="bank%d" % (n % ROTATING_BANKS))

        vec_rows = keep.tile([P, GROUP], BF16, name="vec_rows")
        nc.gpsimd.memset(vec_rows[:].bitcast(I32), 0)
        ident = keep.tile([P, P], F32, name="ident")
        make_identity(nc, ident[:])

        zero_bias = keep.tile([P, 1], F32, name="zero_bias")
        nc.scalar.activation(out=zero_bias[:], in_=ident[:, 0:1], func=ACT.Tanh, scale=0.0)

        h_packed = keep.tile([P, 1, B], U8, name="h_packed", align_bytes=64)
        h_later = keep.tile([P, G - 1, B], U8, name="h_later", align_bytes=64)
        c_first = keep.tile([P, 2, D], U8, name="c_first", align_bytes=64)
        c_later = keep.tile([P, 2 * (G - 1), D], U8, name="c_later", align_bytes=64)
        for plane in (h_packed, h_later, c_first, c_later):
            nc.vector.memset(plane[:].rearrange("p v n -> p (v n)").bitcast(I32), 0)
        c_plane = [c_first[:, n, :] for n in range(2)] + [c_later[:, n, :] for n in range(2 * (G - 1))]

        x_sb = [keep.tile([P, 2, K], BF16, name="x%d" % h) for h in range(HALVES)]
        lex_sb = [keep.tile([P, 2, D], BF16, name="lex%d" % h) for h in range(HALVES)]
        h_sb = [keep.tile([P, 2 * B], U8, name="h%d" % v) for v in range(G)]
        c_sb = [keep.tile([P, 2, 2 * D], U8, name="c%d" % v, align_bytes=64) for v in range(G)]
        doc_vecs = keep.tile([P, 2 * VEC_ROWS, PACK], F32, name="doc_vecs")
        doc_gain_sb, doc_bias_sb = doc_vecs[:, 0:VEC_ROWS, :], doc_vecs[:, VEC_ROWS : 2 * VEC_ROWS, :]
        y_plane = keep.tile([P, 2, G * R], U8, name="y_plane", align_bytes=64)

        h_ordered = [keep.tile([P, PACK, 2 * P, 2], U8, name="hw%d" % v, align_bytes=64) for v in range(G)]
        packed_ordered = keep.tile([P, PACK, 2 * P], U8, name="packed_ordered", align_bytes=64)
        h_plane = [packed_ordered] + [h_later[:, n, :].rearrange("p (t m) -> p t m", t=PACK) for n in range(G - 1)]

        vec_bank = psum.tile([P, GROUP], F32, name="vec_bank")
        vecs_turned = vec_bank[:, 0 : 2 * P].bitcast(BF16).rearrange("p (u j e) -> p j u e", u=2, e=2)

        def half_rows(tensor, h):
            r0 = (h % 2) * HALF
            return tensor[h // 2, r0 : r0 + HALF, :]

        def load_x(h):
            nc.sync.dma_start(out=x_sb[h][:], in_=half_rows(x, h).rearrange("(i b) k -> i b k", b=2))

        def load_lex(h):
            nc.sync.dma_start(out=lex_sb[h][:], in_=half_rows(lex, h).rearrange("(b r) d -> r b d", b=2))

        def load_h(v):
            nc.sync.dma_start(out=h_sb[v][:].bitcast(I32), in_=h_words[v].bitcast(I32))

        def load_c(v):
            nc.sync.dma_start(
                out=c_sb[v][:].bitcast(I32), in_=c_words[2 * v : 2 * v + 2].rearrange("g p n -> p g n").bitcast(I32)
            )

        def load_c_planes(planes, scales):
            for q in range(QUADRANTS):
                nc.sync.dma_start(
                    out=planes[32 * q : 32 * q + 4].bitcast(I32),
                    in_=scales[:, 4 * q : 4 * q + 4, :].rearrange("g r n -> r g n").bitcast(I32),
                )

        def load_h_packed():
            for q in range(QUADRANTS):
                nc.sync.dma_start(
                    out=h_packed[32 * q : 32 * q + 4 * G, 0, :].bitcast(I32),
                    in_=h_scales[:, 4 * q : 4 * q + 4, :].bitcast(I32),
                )

        def load_vecs():
            for n, vec in enumerate((bit_gain, doc_gain, doc_bias)):
                nc.sync.dma_start(
                    out=vec_rows[VEC_ROWS * n : VEC_ROWS * (n + 1), :], in_=vec.rearrange("v (g k) -> (v g) k", g=2)
                )

        def spread_h_scales(v):
            flat = packed_ordered[:].rearrange("p t m -> p (t m)")
            for q in range(QUADRANTS):
                nc.sync.dma_start(
                    out=h_later[32 * q : 32 * q + 4, v - 1, :].bitcast(I32),
                    in_=flat[32 * q + 4 * v : 32 * q + 4 * v + 4, :].bitcast(I32),
                )

        x_bank, x_grouped, x_mx, p_bank, tanh_sb, z_grouped, z_mx = {}, {}, {}, {}, {}, {}, {}
        s_bank, sum_sb, sum_bank, y_turned, y_bank, y_grouped = {}, {}, {}, {}, {}, {}

        def turn_pairs(bank, first_slot, rows):
            words = rows.bitcast(F32)
            for u in range(2):
                slot = first_slot + u
                nc.tensor.transpose(bank[:, slot * P : (slot + 1) * P], words[:, u : 2 * P : 2], ident[:])

        def copy_doc_vecs():
            nc.scalar.copy(
                out=doc_vecs[:].rearrange("p j (u e) -> p j u e", u=2), in_=vecs_turned[:, VEC_ROWS : 3 * VEC_ROWS]
            )

        def turn_x(h):
            x_bank[h] = next_bank()
            for b in range(2):
                turn_pairs(x_bank[h], 2 * b, x_sb[h][:, b, :])

        def group_x(h):
            x_grouped[h] = work.tile([P, HALF * PACK], BF16, name="xg%d" % h, tag="xg", bufs=2, align_bytes=64)
            nc.scalar.copy(
                out=x_grouped[h][:].bitcast(F32).rearrange("p (i b u) -> p i b u", b=2, u=2),
                in_=x_bank[h][:].rearrange("p (b u i) -> p i b u", b=2, u=2),
            )

        def quantize(src, width, tag, n):
            codes = work.tile([P, width], U32, name="%s_codes%d" % (tag, n), tag=tag + "_codes", align_bytes=64)
            plane = work.tile([P, width], U8, name="%s_plane%d" % (tag, n), tag=tag + "_plane", align_bytes=64)
            nc.vector.quantize_mx(out=codes[:].bitcast(FP8X4), scales=plane[:], in_=src[:])
            return codes, plane

        def quantize_x(h):
            x_mx[h] = quantize(x_grouped[h], HALF, "x", h)

        def reorder_h_words(v, g):
            cols = slice(g * P, (g + 1) * P)
            nc.vector.tensor_copy(
                out=h_ordered[v][:, :, cols, :],
                in_=h_sb[v][:].rearrange("p (m t b) -> p t m b", t=PACK, b=2)[:, :, cols, :],
            )

        def reorder_h_scales(g):
            cols = slice(g * P, (g + 1) * P)
            nc.vector.tensor_copy(
                out=packed_ordered[:, :, cols], in_=h_packed[:, 0, :].rearrange("p (m t) -> p t m", t=PACK)[:, :, cols]
            )

        def project(s):
            h, g = divmod(s, 2)
            words = h_ordered[h // 2][:].rearrange("p t m b -> p t (m b)")
            codes, plane = x_mx[h]
            for u in range(2):
                p_bank[s, u] = next_bank()
                for e in range(2):
                    t = 2 * u + e
                    nc.tensor.matmul_mx(
                        out=p_bank[s, u][:, e * HALF : (e + 1) * HALF],
                        lhsT=words[:, t, 2 * P * g : 2 * P * (g + 1)].bitcast(FP4X4),
                        lhsT_scale=h_plane[h // 2][:, t, P * g : P * (g + 1)],
                        rhs=codes[:].bitcast(FP8X4),
                        rhs_scale=plane[:],
                        start=True,
                        stop=True,
                    )

        def soften(s):
            tanh_sb[s] = work.tile([P, 2, HALF, 2], F32, name="tanh%d" % s, tag="tanh", bufs=4)
            for u in range(2):
                nc.scalar.activation(
                    out=tanh_sb[s][:, u],
                    in_=p_bank[s, u][:].rearrange("p (e r) -> p r e", e=2),
                    func=ACT.Tanh,
                    bias=zero_bias[:],
                )

        def apply_gain(s):
            h, g = divmod(s, 2)
            if g == 0:
                z_grouped[h] = work.tile([P, 2 * HALF * PACK], BF16, name="z%d" % h, tag="z", bufs=2, align_bytes=64)
            z = z_grouped[h][:, g * HALF * PACK : (g + 1) * HALF * PACK]
            nc.vector.tensor_tensor(
                out=z.rearrange("p (r u e) -> p r u e", u=2, e=2),
                in0=tanh_sb[s][:].rearrange("p u r e -> p r u e"),
                in1=vecs_turned[:, 2 * (h // 2) + g].unsqueeze(1).to_broadcast([P, HALF, 2, 2]),
                op=ALU.mult,
            )

        def quantize_z(h):
            z_mx[h] = quantize(z_grouped[h], 2 * HALF, "z", h)

        def score(s):
            h, dg = divmod(s, 2)
            v = h // 2
            codes, plane = z_mx[h]
            for b in range(2):
                s_bank[s, b] = next_bank()
                for g in range(2):
                    cols = slice(g * HALF + b * P, g * HALF + (b + 1) * P)
                    nc.tensor.matmul_mx(
                        out=s_bank[s, b][:],
                        lhsT=codes[:, cols].bitcast(FP8X4),
                        lhsT_scale=plane[:, cols],
                        rhs=c_sb[v][:, g, 2 * GROUP * dg : 2 * GROUP * (dg + 1)].bitcast(FP4X4),
                        rhs_scale=c_plane[2 * v + g][:, GROUP * dg : GROUP * (dg + 1)],
                        start=(g == 0),
                        stop=(g == 1),
                    )

        def add_lex(s):
            h, dg = divmod(s, 2)
            sum_sb[s] = work.tile([P, 2, GROUP], F32, name="sum%d" % s, tag="sum")
            for b in range(2):
                docs = lex_sb[h][:, b, GROUP * dg : GROUP * (dg + 1)]
                nc.vector.tensor_tensor(
                    out=sum_sb[s][:, b, :].rearrange("r (t c i) -> r c t i", t=PACK, i=LINE),
                    in0=s_bank[s, b][:].rearrange("r (c i t) -> r c t i", t=PACK, i=LINE),
                    in1=docs.rearrange("r (c i t) -> r c t i", t=PACK, i=LINE),
                    op=ALU.add,
                )

        def turn_sum(s):
            for u in range(2):
                sum_bank[s, u] = next_bank()
                for e in range(2):
                    t = 2 * u + e
                    for b in range(2):
                        slot = 2 * e + b
                        nc.tensor.transpose(
                            sum_bank[s, u][:, slot * P : (slot + 1) * P], sum_sb[s][:, b, t * P : (t + 1) * P], ident[:]
                        )

        def finish(s):
            h, dg = divmod(s, 2)
            row = 2 * (h // 2) + dg
            y_turned[s] = work.tile([P, PACK, HALF], F32, name="yt%d" % s, tag="yt", bufs=4)
            for t in range(PACK):
                u, e = divmod(t, 2)
                dst, src = y_turned[s][:, t, :], sum_bank[s, u][:, e * HALF : (e + 1) * HALF]
                gain, bias = doc_gain_sb[:, row, t : t + 1], doc_bias_sb[:, row, t : t + 1]
                if u == 1 and s >= STEPS - TAIL_STEPS:
                    nc.vector.tensor_scalar(out=dst, in0=src, scalar1=gain, scalar2=bias, op0=ALU.mult, op1=ALU.add)
                else:
                    nc.scalar.activation(out=dst, in_=src, func=ACT.Identity, scale=gain, bias=bias)

        def turn_back(s):
            for b in range(2):
                y_bank[s, b] = next_bank()
                for t in range(PACK):
                    nc.tensor.transpose(
                        y_bank[s, b][:, t * P : (t + 1) * P], y_turned[s][:, t, b * P : (b + 1) * P], ident[:]
                    )

        def store_y(s):
            h, dg = divmod(s, 2)
            for b in range(2):
                y = work.tile([P, GROUP], F32, name="y%d_%d" % (s, b), tag="y", bufs=4)
                on_vector = b == 1 and s % VECTOR_COPY_PERIOD == VECTOR_COPY_PERIOD - 1
                copy = nc.vector.tensor_copy if on_vector else nc.scalar.copy
                copy(
                    out=y[:].rearrange("r (p t) -> r p t", t=PACK),
                    in_=y_bank[s, b][:].rearrange("r (t p) -> r p t", t=PACK),
                )
                dst = half_rows(out_0, h)[b * P : (b + 1) * P, GROUP * dg : GROUP * (dg + 1)]
                nc.sync.dma_start(out=dst, in_=y[:])

        def group_y(s):
            y_grouped[s] = work.tile([P, HALF * PACK], BF16, name="yg%d" % s, tag="yg", align_bytes=64)
            if s < STEPS - TAIL_STEPS:
                nc.gpsimd.tensor_scalar(
                    out=y_grouped[s][:].rearrange("p (r t) -> p r t", t=PACK),
                    in0=y_turned[s][:].rearrange("p t r -> p r t"),
                    scalar1=1.0,
                    scalar2=-0.0,
                    op0=ALU.mult,
                    op1=ALU.add,
                )
            else:
                nc.vector.tensor_copy(
                    out=y_grouped[s][:].rearrange("p (c i t) -> p c t i", t=PACK, i=LINE),
                    in_=y_turned[s][:].rearrange("p t (c i) -> p c t i", i=LINE),
                )

        def store_planes(s):
            h, dg = divmod(s, 2)
            cols = slice(h * HALF, (h + 1) * HALF)
            codes = work.tile([P, HALF], U32, name="y_codes%d" % s, tag="y_codes", align_bytes=64)
            nc.vector.quantize_mx(out=codes[:].bitcast(FP8X4), scales=y_plane[:, dg, cols], in_=y_grouped[s][:])
            nc.sync.dma_start(
                out=out_1[dg, :, cols, :].rearrange("p m t -> p (m t)").bitcast(I32), in_=codes[:].bitcast(I32)
            )
            if (s + 1) % (STEPS // G) == 0:
                view = slice((h // 2) * R, (h // 2 + 1) * R)
                for q in range(QUADRANTS):
                    nc.sync.dma_start(
                        out=out_2[:, 4 * q : 4 * q + 4, view].rearrange("g r m -> r g m").bitcast(I32),
                        in_=y_plane[32 * q : 32 * q + 4, :, view].bitcast(I32),
                    )

        load_x(0)
        load_h(0)
        load_h_packed()
        load_vecs()
        load_x(1)
        load_h(1)
        load_x(2)
        load_c_planes(c_first, c_scales[0:2])
        load_c(0)
        load_lex(0)

        turn_x(0)
        turn_pairs(vec_bank, 0, vec_rows[:])
        reorder_h_words(0, 0)
        group_x(0)
        copy_doc_vecs()
        reorder_h_scales(0)
        quantize_x(0)
        reorder_h_words(0, 1)
        reorder_h_scales(1)

        spread_h_scales(1)
        load_h(2)
        load_x(3)
        load_lex(1)
        load_x(4)
        spread_h_scales(2)
        spread_h_scales(3)
        load_c_planes(c_later, c_scales[2 : 2 * G])
        load_c(1)
        load_lex(2)
        load_x(5)
        load_h(3)
        load_lex(3)
        load_x(6)
        load_c(2)
        load_lex(4)
        load_x(7)
        load_lex(5)
        load_c(3)
        load_lex(6)
        load_lex(7)

        def live(s):
            return 0 <= s < STEPS

        def project_round(s):
            return s if s < FIRST_LEADING_STEP else s - 1

        for n in range(STEPS + LAG_PLANES):
            s_score, s_finish, s_back, s_planes = n - LAG_SCORE, n - LAG_FINISH, n - LAG_BACK, n - LAG_PLANES
            projected = [s for s in range(STEPS) if project_round(s) == n]
            turned = [h for h in range(1, HALVES) if project_round(2 * h) - 2 == n]
            quantized = [h for h in range(1, HALVES) if project_round(2 * h) - 1 == n]

            if live(s_score):
                score(s_score)
            for s in projected:
                project(s)
            for h in turned:
                turn_x(h)
            if live(s_finish):
                turn_sum(s_finish)
            if live(s_back):
                turn_back(s_back)

            for s in projected:
                soften(s)
            for h in turned:
                group_x(h)
            if live(n - 1) and n % 2 == 0:
                quantize_z(n // 2 - 1)
            if live(s_score):
                add_lex(s_score)
            if live(n) and n >= FIRST_LEADING_STEP:
                apply_gain(n)
            if live(s_back):
                group_y(s_back)
            for h in quantized:
                quantize_x(h)
            for v in range(1, G):
                for g in range(2):
                    if REORDER_ROUND[v] + g == n:
                        reorder_h_words(v, g)
            if n < FIRST_LEADING_STEP:
                apply_gain(n)
            if live(s_finish):
                finish(s_finish)
            if live(s_planes):
                store_planes(s_planes)
            if live(s_back):
                store_y(s_back)
